import numpy as np
import ml_dtypes


def mxq(x, axis, fmt="e4m3"):
    dtype, down = {"e4m3": (ml_dtypes.float8_e4m3fn, 7), "e5m2": (ml_dtypes.float8_e5m2, 14)}[fmt]
    v = np.moveaxis(np.asarray(x, np.float32).astype(ml_dtypes.bfloat16).astype(np.float64), axis, -1)
    blocks = v.reshape(v.shape[:-1] + (-1, 32))
    amax = np.abs(blocks).max(-1, keepdims=True)
    byte = np.maximum(np.where(amax > 0, np.frexp(amax)[1] - 1 + 127, 0) - down, 1)
    scale = np.exp2(byte - 127.0)
    codes = (blocks / scale).astype(np.float32).astype(dtype).astype(np.float64)
    return np.moveaxis((codes * scale).reshape(v.shape), -1, axis)


WIDE = False


def mx_kscale(k):
    if not WIDE:
        return np.ones(k)
    levels = np.array([10, -10, 5, -5, 0])
    if k % 512:
        return np.exp2(np.random.permutation(np.resize(levels, k // 32))).repeat(32)
    a = np.empty((k // 512, 16))
    for p in range(k // 512):
        a[p, :8] = np.random.permutation(np.resize(levels, 8))
        for g in range(8):
            far = levels[np.abs(levels - a[p, g]) >= 10]
            a[p, g + 8] = far[np.random.randint(len(far))]
    return np.exp2(a.ravel()).repeat(32)


def f64(x):
    return np.asarray(x).astype(np.float64)


def striped(idx):
    return np.tile(idx.reshape(-1, 16).T, (8, 1)).astype(np.uint16)


def unstriped(offs):
    return offs[:16].T.reshape(-1).astype(np.int64)


E2M1 = np.array([0.0, 0.5, 1.0, 1.5, 2.0, 3.0, 4.0, 6.0, -0.0, -0.5, -1.0, -1.5, -2.0, -3.0, -4.0, -6.0])


def pack_weight(w, fmt):
    k, n = w.shape
    w = f64(np.asarray(w, np.float32).astype(ml_dtypes.bfloat16)).reshape(k // 32, 32, n)
    amax = np.abs(w).max(1)
    if fmt == "e4m3":
        byte = np.frexp(amax)[1] - 1 + 127 - 7
    else:
        mant, ex = np.frexp(amax / 6.0)
        byte = np.where(mant > 0.5, ex, ex - 1) + 127
    byte = np.clip(np.where(amax > 0, byte, 1), 1, 254)
    scaled = (w * np.exp2(127.0 - byte)[:, None, :]).reshape(k, n).astype(np.float32)
    by_word = np.ascontiguousarray(scaled.reshape(k // 512, 128, 4, n).transpose(0, 1, 3, 2))
    if fmt == "e4m3":
        words = by_word.astype(ml_dtypes.float8_e4m3fn).view(np.uint8)
    else:
        c = by_word.astype(ml_dtypes.float4_e2m1fn).view(np.uint8) & 0xF
        words = (c[..., 0::2] | (c[..., 1::2] << 4)).reshape(k // 512, 128, 2 * n)
    return np.ascontiguousarray(words), np.ascontiguousarray(byte.astype(np.uint8).reshape(k // 512, 16, n))


def unpack_weight(words, scales, fmt):
    g, _, n = scales.shape
    words = np.ascontiguousarray(words).reshape(g, 128, n, -1)
    if fmt == "e4m3":
        vals = words.view(ml_dtypes.float8_e4m3fn).astype(np.float64)
    else:
        nib = np.empty((g, 128, n, 4), np.uint8)
        nib[..., 0::2] = words & 0xF
        nib[..., 1::2] = words >> 4
        vals = E2M1[nib]
    vals = vals * np.repeat(np.exp2(scales.astype(np.float64) - 127.0), 8, axis=1)[..., None]
    return vals.transpose(0, 1, 3, 2).reshape(g * 512, n)


def silu(v):
    return v / (1.0 + np.exp(-np.maximum(v, -700.0)))


K, T, E, C, H, N = 512, 1536, 8, 128, 1024, 128


def by_expert(wq, xq):
    return np.concatenate([wq[e].T @ xq[:, e * C:(e + 1) * C] for e in range(E)], axis=1)


def setup_inputs():
    n = np.random.standard_normal
    s = mx_kscale(K)[:, None]
    u = mx_kscale(H)
    w1 = [pack_weight(m, "e2m1") for m in n((E, K, H)) / np.sqrt(K) / s[None] * u[None, None, :]]
    w2 = [pack_weight(m, "e2m1") for m in n((E, H, N)) / np.sqrt(H) / u[None, :, None]]
    x = pack_weight(n((K, T)) * s, "e4m3")
    return {
        "x_words": x[0],
        "x_scales": x[1],
        "w1_words": np.stack([m[0] for m in w1]),
        "w1_scales": np.stack([m[1] for m in w1]),
        "w2_words": np.stack([m[0] for m in w2]),
        "w2_scales": np.stack([m[1] for m in w2]),
        "gate": np.tile(np.random.uniform(0.2, 1.0, E * C), (N, 1)).astype(np.float32),
        "offs": striped(np.random.permutation(T)[:E * C]),
        "dst": striped(np.random.permutation(T)[:E * C]),
    }


def reference(x_words, x_scales, w1_words, w1_scales, w2_words, w2_scales, gate, offs, dst):
    idx = unstriped(offs)
    w1 = np.stack([unpack_weight(w1_words[e], w1_scales[e], "e2m1") for e in range(E)])
    w2 = np.stack([unpack_weight(w2_words[e], w2_scales[e], "e2m1") for e in range(E)])
    xq = unpack_weight(x_words, x_scales, "e4m3")[:, idx]
    h = silu(by_expert(w1, xq))
    y = by_expert(w2, mxq(h, 0, "e4m3"))
    out = np.zeros((N, T))
    out[:, unstriped(dst)] = f64(gate) * y
    return out

@@ -1,0 +1,205 @@
+from contextlib import ExitStack
+
+import concourse.mybir as mybir
+from concourse.masks import make_identity
+
+K, T, E, C, H, N = 512, 1536, 8, 128, 1024, 128
+SLOTS = E * C
+FLOPS = 2 * SLOTS * (K * H + H * N)
+
+F32 = mybir.dt.float32
+BF16 = mybir.dt.bfloat16
+I32 = mybir.dt.int32
+U32 = mybir.dt.uint32
+U16 = mybir.dt.uint16
+U8 = mybir.dt.uint8
+FP8X4 = mybir.dt.float8_e4m3fn_x4
+FP4X4 = mybir.dt.float4_e2m1fn_x4
+SILU = mybir.ActivationFunctionType.Silu
+MULT = mybir.AluOpType.mult
+
+P = 128
+PASS = 512
+PASSES = H // PASS
+GATHERS = ((0, 192, 0, "bw"), (192, 512, 0, "bw"), (512, 1024, 2, "bw"))
+SCALE_GROUPS = ((0, 1, 2, 3), (4, 5, 6, 7))
+WORD_GROUPS = ((0,), (1,), (2, 3), (4, 5), (6, 7))
+Y_GROUPS = ((0,), (1,), (2,), (3,), (4,), (5,), (6,), (7,))
+SCATTER_ENDS = (256, 448, 640, 832, 1024)
+TURN_ON_SCALAR = (6, 7)
+LAG_TURN, LAG_QUANT, LAG_SCATTER = (1, 3, 1)
+
+
+def tile_moe_two_mlp_silu_kernel(
+    tc, x_words, x_scales, w1_words, w1_scales, w2_words, w2_scales, gate, offs, dst, out
+):
+    nc = tc.nc
+    with ExitStack() as ctx:
+        held = ctx.enter_context(tc.tile_pool(name="held", bufs=1))
+        ring = ctx.enter_context(tc.tile_pool(name="ring", bufs=8))
+        psum_a = ctx.enter_context(tc.psum_pool(name="psum_a", bufs=2))
+        psum_t = ctx.enter_context(tc.psum_pool(name="psum_t", bufs=2))
+        psum_y = ctx.enter_context(tc.psum_pool(name="psum_y", bufs=2))
+
+        offs_sb = held.tile([P, SLOTS // 16], U16, name="offs_sb")
+        dst_sb = held.tile([P, SLOTS // 16], U16, name="dst_sb")
+        tok_words = held.tile([P, T], I32, name="tok_words", align_bytes=64)
+        tok_scales = held.tile([P, T], U8, name="tok_scales", align_bytes=64)
+        slot_words = held.tile([P, SLOTS], U32, name="slot_words", align_bytes=64)
+        slot_scales = held.tile([P, SLOTS], U8, name="slot_scales", align_bytes=64)
+        w1w = [held.tile([P, len(grp), 2 * H], U8, name="w1w%d" % g, align_bytes=64) for g, grp in enumerate(WORD_GROUPS)]
+        w1w_of = {e: w1w[g][:, e - grp[0], :] for g, grp in enumerate(WORD_GROUPS) for e in grp}
+        w1s = [held.tile([P, len(grp), H], U8, name="w1s%d" % g, align_bytes=64) for g, grp in enumerate(SCALE_GROUPS)]
+        w1s_of = {e: w1s[g][:, e - grp[0], :] for g, grp in enumerate(SCALE_GROUPS) for e in grp}
+        w2w = held.tile([P, E * PASSES, 2 * N], U8, name="w2w", align_bytes=64)
+        w2s = held.tile([P, E * PASSES, N], U8, name="w2s", align_bytes=64)
+        gate_sb = held.tile([P, SLOTS], F32, name="gate_sb")
+        y_sb = held.tile([P, SLOTS], F32, name="y_sb")
+        out_sb = held.tile([P, T], F32, name="out_sb")
+        ident = held.tile([P, P], F32, name="ident", align_bytes=64)
+        zero = held.tile([P, 2], F32, name="zero")
+
+        def load_plane(queue, plane, rows):
+            for r in range(4):
+                queue.dma_start(out=plane[r:P:32], in_=rows[r])
+
+        def load_w1_words(queue, g):
+            src = w1_words.bitcast(I32)[WORD_GROUPS[g][0]:WORD_GROUPS[g][-1] + 1, 0].rearrange("e p b -> p e b")
+            queue.dma_start(out=w1w[g][:].bitcast(I32), in_=src)
+
+        def load_w1_scales(queue, g):
+            src = w1_scales.bitcast(I32)[SCALE_GROUPS[g][0]:SCALE_GROUPS[g][-1] + 1, 0]
+            load_plane(queue, w1s[g][:].bitcast(I32), src.rearrange("e (q r) i -> r q e i", r=4))
+
+        def load_w2_words(queue, lo, hi):
+            src = w2_words.bitcast(I32)[lo:hi].rearrange("e s p b -> p (e s) b")
+            queue.dma_start(out=w2w[:, lo * PASSES:hi * PASSES, :].bitcast(I32), in_=src)
+
+        nc.vector.memset(tok_scales[:].bitcast(I32), 0)
+        nc.vector.memset(zero[:], 0.0)
+        nc.vector.memset(w1s[0][:].bitcast(I32), 0)
+        nc.vector.memset(w1s[1][:].bitcast(I32), 0)
+        nc.vector.memset(w2s[:].bitcast(I32), 0)
+        nc.scalar.activation(out=out_sb[:], in_=zero[:, 0:1].to_broadcast([P, T]), func=SILU)
+        make_identity(nc, ident[:])
+        nc.sync.dma_start(offs_sb[:], offs)
+        nc.sync.dma_start(dst_sb[:], dst)
+        load_plane(nc.sync, tok_scales[:].bitcast(I32), x_scales.bitcast(I32)[0].rearrange("(q r) t -> r q t", r=4))
+        nc.sync.dma_start(out=tok_words[:], in_=x_words[0].rearrange("p t r -> p (t r)").bitcast(I32))
+        load_w1_words(nc.sync, 0)
+        load_w1_scales(nc.sync, 0)
+        load_w1_words(nc.sync, 1)
+        load_w1_words(nc.sync, 2)
+        load_w2_words(nc.sync, 0, 2)
+        load_plane(nc.sync, w2s[:].bitcast(I32), w2_scales.bitcast(I32).rearrange("e s (q r) n -> r q (e s) n", r=4))
+        load_w1_words(nc.sync, 3)
+        load_w1_words(nc.sync, 4)
+        nc.sync.dma_start(out=gate_sb[:, 0:256], in_=gate[:, 0:256])
+        load_w1_scales(nc.sync, 1)
+        load_w2_words(nc.sync, 2, 8)
+        nc.sync.dma_start(out=gate_sb[:, 256:1024], in_=gate[:, 256:1024])
+
+        def gather(lo, hi, sorts):
+            picks = offs_sb[:, lo // 16:hi // 16]
+            if "b" in sorts:
+                nc.vector.tensor_copy(slot_scales[:, lo:hi], tok_scales[:].indirect(picks))
+            if "w" in sorts:
+                nc.vector.tensor_copy(slot_words[:, lo:hi], tok_words[:].bitcast(U32).indirect(picks))
+
+        h_of = {}
+        grouped_of = {}
+        codes_of = {}
+        y_of = {}
+
+        def first_layer(e):
+            cols = slice(e * C, (e + 1) * C)
+            h = ring.tile([P, H], BF16, name="h", align_bytes=64)
+            sums = psum_a.tile([P, PASSES, PASS], F32, name="sums")
+            for s in range(PASSES):
+                a = sums[:, s, :]
+                nc.tensor.matmul_mx(
+                    out=a,
+                    lhsT=slot_words[:, cols].bitcast(FP8X4),
+                    lhsT_scale=slot_scales[:, cols],
+                    rhs=w1w_of[e][:, 2 * s * PASS:2 * (s + 1) * PASS].bitcast(FP4X4),
+                    rhs_scale=w1s_of[e][:, s * PASS:(s + 1) * PASS],
+                    start=True,
+                    stop=True,
+                )
+                nc.scalar.activation(
+                    out=h[:, s * PASS:(s + 1) * PASS].rearrange("c (u m d) -> c u m d", u=2, d=2),
+                    in_=a.rearrange("c (m u d) -> c u m d", u=2, d=2),
+                    func=SILU,
+                )
+            h_of[e] = h
+
+        def turn(e):
+            pairs = h_of[e][:].bitcast(F32)
+            turned = psum_t.tile([P, PASSES, 2, C], F32, name="turned")
+            for s in range(PASSES):
+                for u in range(2):
+                    b = 2 * s + u
+                    nc.tensor.transpose(turned[:, s, u, :], pairs[:, b * P:(b + 1) * P], ident[:])
+            grouped = ring.tile([P, PASSES * C * 4], BF16, name="grouped", align_bytes=64)
+            to = grouped[:].bitcast(F32).rearrange("p (s c u) -> p s c u", s=PASSES, u=2)
+            frm = turned[:].rearrange("p s u c -> p s c u")
+            if e in TURN_ON_SCALAR:
+                nc.scalar.copy(out=to, in_=frm)
+            else:
+                nc.vector.tensor_copy(out=to, in_=frm)
+            grouped_of[e] = grouped
+
+        def quantise(e):
+            codes = ring.tile([P, PASSES * C], U32, name="codes", align_bytes=64)
+            scales = ring.tile([P, PASSES * C], U8, name="scales", align_bytes=64)
+            nc.vector.quantize_mx(out=codes[:].bitcast(FP8X4), scales=scales[:], in_=grouped_of[e][:])
+            codes_of[e] = (codes, scales)
+
+        def second_layer(e):
+            codes, scales = codes_of[e]
+            group = [grp for grp in Y_GROUPS if e in grp][0]
+            if e == group[0]:
+                y_of[group] = psum_y.tile([P, len(group) * C], F32, name="y")
+            y = y_of[group]
+            place = (e - group[0]) * C
+            for s in range(PASSES):
+                nc.tensor.matmul_mx(
+                    out=y[:, place:place + C],
+                    lhsT=w2w[:, e * PASSES + s, :].bitcast(FP4X4),
+                    lhsT_scale=w2s[:, e * PASSES + s, :],
+                    rhs=codes[:, s * C:(s + 1) * C].bitcast(FP8X4),
+                    rhs_scale=scales[:, s * C:(s + 1) * C],
+                    start=(s == 0),
+                    stop=(s == PASSES - 1),
+                )
+            if e == group[-1]:
+                nc.scalar.copy(out=y_sb[:, group[0] * C:(e + 1) * C], in_=y[:])
+                return (e + 1) * C
+            return group[0] * C
+
+        def scatter(lo, hi):
+            places = dst_sb[:, lo // 16:hi // 16]
+            nc.vector.tensor_tensor(out_sb[:].indirect(places), y_sb[:, lo:hi], gate_sb[:, lo:hi], MULT)
+
+        scattered = 0
+        done = 0
+        done_at = {}
+        for step in range(E + LAG_QUANT + LAG_SCATTER):
+            for lo, hi, at, sorts in GATHERS:
+                if at == step:
+                    gather(lo, hi, sorts)
+            if step < E:
+                first_layer(step)
+            if 0 <= step - LAG_TURN < E:
+                turn(step - LAG_TURN)
+            if 0 <= step - LAG_QUANT < E:
+                quantise(step - LAG_QUANT)
+                done = second_layer(step - LAG_QUANT)
+            done_at[step] = done
+            for end in SCATTER_ENDS:
+                if scattered < end <= done_at.get(step - LAG_SCATTER, 0):
+                    scatter(scattered, end)
+                    scattered = end
+        assert scattered == SLOTS
+
+        nc.sync.dma_start(out=out[:, 0:1536], in_=out_sb[:, 0:1536])

@@ -22,12 +22,15 @@ P = 128
 PASS = 512
 PASSES = H // PASS
 GATHERS = ((0, 192, 0, "bw"), (192, 512, 0, "bw"), (512, 1024, 2, "bw"))
-SCALE_GROUPS = ((0, 1, 2, 3), (4, 5, 6, 7))
+SCALE_GROUPS = ((0, 1), (2, 3, 4, 5, 6, 7))
 WORD_GROUPS = ((0,), (1,), (2, 3), (4, 5), (6, 7))
-Y_GROUPS = ((0,), (1,), (2,), (3,), (4,), (5,), (6,), (7,))
+Y_GROUPS = ((0, 1), (2, 3), (4, 5), (6,), (7,))
 SCATTER_ENDS = (256, 448, 640, 832, 1024)
-TURN_ON_SCALAR = (6, 7)
-LAG_TURN, LAG_QUANT, LAG_SCATTER = (1, 3, 1)
+TURN_ON_SCALAR = (0, 3, 5, 7)
+HALVED = (0, 3, 4, 5)
+Y_ON_VECTOR = (0, 2, 3, 5, 6)
+LAG_SECOND = 2
+LAG_TURN, LAG_QUANT, LAG_SCATTER = (1, 2, 2)
 
 
 def tile_moe_two_mlp_silu_kernel(
@@ -37,9 +40,9 @@ def tile_moe_two_mlp_silu_kernel(
     with ExitStack() as ctx:
         held = ctx.enter_context(tc.tile_pool(name="held", bufs=1))
         ring = ctx.enter_context(tc.tile_pool(name="ring", bufs=8))
-        psum_a = ctx.enter_context(tc.psum_pool(name="psum_a", bufs=2))
+        psum_a = ctx.enter_context(tc.psum_pool(name="psum_a", bufs=5))
         psum_t = ctx.enter_context(tc.psum_pool(name="psum_t", bufs=2))
-        psum_y = ctx.enter_context(tc.psum_pool(name="psum_y", bufs=2))
+        psum_y = ctx.enter_context(tc.psum_pool(name="psum_y", bufs=1))
 
         offs_sb = held.tile([P, SLOTS // 16], U16, name="offs_sb")
         dst_sb = held.tile([P, SLOTS // 16], U16, name="dst_sb")
@@ -80,24 +83,24 @@ def tile_moe_two_mlp_silu_kernel(
         nc.vector.memset(w1s[0][:].bitcast(I32), 0)
         nc.vector.memset(w1s[1][:].bitcast(I32), 0)
         nc.vector.memset(w2s[:].bitcast(I32), 0)
-        nc.scalar.activation(out=out_sb[:], in_=zero[:, 0:1].to_broadcast([P, T]), func=SILU)
         make_identity(nc, ident[:])
         nc.sync.dma_start(offs_sb[:], offs)
+        nc.scalar.activation(out=out_sb[:], in_=zero[:, 0:1].to_broadcast([P, T]), func=SILU)
         nc.sync.dma_start(dst_sb[:], dst)
         load_plane(nc.sync, tok_scales[:].bitcast(I32), x_scales.bitcast(I32)[0].rearrange("(q r) t -> r q t", r=4))
         nc.sync.dma_start(out=tok_words[:], in_=x_words[0].rearrange("p t r -> p (t r)").bitcast(I32))
-        load_w1_words(nc.sync, 0)
+        load_w1_words(nc.scalar, 0)
         load_w1_scales(nc.sync, 0)
         load_w1_words(nc.sync, 1)
         load_w1_words(nc.sync, 2)
-        load_w2_words(nc.sync, 0, 2)
+        load_w1_scales(nc.scalar, 1)
         load_plane(nc.sync, w2s[:].bitcast(I32), w2_scales.bitcast(I32).rearrange("e s (q r) n -> r q (e s) n", r=4))
+        load_w2_words(nc.sync, 0, 4)
         load_w1_words(nc.sync, 3)
-        load_w1_words(nc.sync, 4)
         nc.sync.dma_start(out=gate_sb[:, 0:256], in_=gate[:, 0:256])
-        load_w1_scales(nc.sync, 1)
-        load_w2_words(nc.sync, 2, 8)
+        load_w1_words(nc.sync, 4)
         nc.sync.dma_start(out=gate_sb[:, 256:1024], in_=gate[:, 256:1024])
+        load_w2_words(nc.sync, 4, 8)
 
         def gather(lo, hi, sorts):
             picks = offs_sb[:, lo // 16:hi // 16]
@@ -114,11 +117,10 @@ def tile_moe_two_mlp_silu_kernel(
         def first_layer(e):
             cols = slice(e * C, (e + 1) * C)
             h = ring.tile([P, H], BF16, name="h", align_bytes=64)
-            sums = psum_a.tile([P, PASSES, PASS], F32, name="sums")
             for s in range(PASSES):
-                a = sums[:, s, :]
+                a = psum_a.tile([P, PASS], F32, name="a")
                 nc.tensor.matmul_mx(
-                    out=a,
+                    out=a[:],
                     lhsT=slot_words[:, cols].bitcast(FP8X4),
                     lhsT_scale=slot_scales[:, cols],
                     rhs=w1w_of[e][:, 2 * s * PASS:2 * (s + 1) * PASS].bitcast(FP4X4),
@@ -128,31 +130,40 @@ def tile_moe_two_mlp_silu_kernel(
                 )
                 nc.scalar.activation(
                     out=h[:, s * PASS:(s + 1) * PASS].rearrange("c (u m d) -> c u m d", u=2, d=2),
-                    in_=a.rearrange("c (m u d) -> c u m d", u=2, d=2),
+                    in_=a[:].rearrange("c (m u d) -> c u m d", u=2, d=2),
                     func=SILU,
                 )
             h_of[e] = h
 
+        def pieces(e):
+            return [(0,), (1,)] if e in HALVED else [(0, 1)]
+
         def turn(e):
             pairs = h_of[e][:].bitcast(F32)
-            turned = psum_t.tile([P, PASSES, 2, C], F32, name="turned")
-            for s in range(PASSES):
-                for u in range(2):
-                    b = 2 * s + u
-                    nc.tensor.transpose(turned[:, s, u, :], pairs[:, b * P:(b + 1) * P], ident[:])
             grouped = ring.tile([P, PASSES * C * 4], BF16, name="grouped", align_bytes=64)
-            to = grouped[:].bitcast(F32).rearrange("p (s c u) -> p s c u", s=PASSES, u=2)
-            frm = turned[:].rearrange("p s u c -> p s c u")
-            if e in TURN_ON_SCALAR:
-                nc.scalar.copy(out=to, in_=frm)
-            else:
-                nc.vector.tensor_copy(out=to, in_=frm)
+            for piece in pieces(e):
+                turned = psum_t.tile([P, len(piece), 2, C], F32, name="turned")
+                for s in piece:
+                    for u in range(2):
+                        b = 2 * s + u
+                        nc.tensor.transpose(turned[:, s - piece[0], u, :], pairs[:, b * P:(b + 1) * P], ident[:])
+                words = grouped[:].bitcast(F32)[:, piece[0] * 2 * C:(piece[-1] + 1) * 2 * C]
+                to = words.rearrange("p (s c u) -> p s c u", s=len(piece), u=2)
+                frm = turned[:].rearrange("p s u c -> p s c u")
+                if e in TURN_ON_SCALAR:
+                    nc.scalar.copy(out=to, in_=frm)
+                else:
+                    nc.vector.tensor_copy(out=to, in_=frm)
             grouped_of[e] = grouped
 
         def quantise(e):
             codes = ring.tile([P, PASSES * C], U32, name="codes", align_bytes=64)
             scales = ring.tile([P, PASSES * C], U8, name="scales", align_bytes=64)
-            nc.vector.quantize_mx(out=codes[:].bitcast(FP8X4), scales=scales[:], in_=grouped_of[e][:])
+            for piece in pieces(e):
+                lo, hi = piece[0] * C, (piece[-1] + 1) * C
+                nc.vector.quantize_mx(
+                    out=codes[:, lo:hi].bitcast(FP8X4), scales=scales[:, lo:hi], in_=grouped_of[e][:, 4 * lo:4 * hi]
+                )
             codes_of[e] = (codes, scales)
 
         def second_layer(e):
@@ -173,18 +184,19 @@ def tile_moe_two_mlp_silu_kernel(
                     stop=(s == PASSES - 1),
                 )
             if e == group[-1]:
-                nc.scalar.copy(out=y_sb[:, group[0] * C:(e + 1) * C], in_=y[:])
+                cols = slice(group[0] * C, (e + 1) * C)
+                nc.vector.tensor_tensor(y_sb[:, cols], y[:], gate_sb[:, cols], MULT)
                 return (e + 1) * C
             return group[0] * C
 
         def scatter(lo, hi):
             places = dst_sb[:, lo // 16:hi // 16]
-            nc.vector.tensor_tensor(out_sb[:].indirect(places), y_sb[:, lo:hi], gate_sb[:, lo:hi], MULT)
+            nc.vector.tensor_copy(out_sb[:].indirect(places), y_sb[:, lo:hi])
 
         scattered = 0
         done = 0
         done_at = {}
-        for step in range(E + LAG_QUANT + LAG_SCATTER):
+        for step in range(E + LAG_SECOND + LAG_SCATTER):
             for lo, hi, at, sorts in GATHERS:
                 if at == step:
                     gather(lo, hi, sorts)
@@ -194,7 +206,8 @@ def tile_moe_two_mlp_silu_kernel(
                 turn(step - LAG_TURN)
             if 0 <= step - LAG_QUANT < E:
                 quantise(step - LAG_QUANT)
-                done = second_layer(step - LAG_QUANT)
+            if 0 <= step - LAG_SECOND < E:
+                done = second_layer(step - LAG_SECOND)
             done_at[step] = done
             for end in SCATTER_ENDS:
                 if scattered < end <= done_at.get(step - LAG_SCATTER, 0):

@@ -22,14 +22,14 @@ P = 128
 PASS = 512
 PASSES = H // PASS
 GATHERS = ((0, 192, 0, "bw"), (192, 512, 0, "bw"), (512, 1024, 2, "bw"))
-SCALE_GROUPS = ((0, 1), (2, 3, 4, 5, 6, 7))
-WORD_GROUPS = ((0,), (1,), (2, 3), (4, 5), (6, 7))
-Y_GROUPS = ((0, 1), (2, 3), (4, 5), (6,), (7,))
+SCALE_GROUPS = ((0, 1, 2), (3, 4, 5, 6, 7))
+WORD_GROUPS = ((0,), (1, 2), (3, 4), (5, 6, 7))
+Y_GROUPS = ((0,), (1,), (2,), (3,), (4,), (5,), (6,), (7,))
 SCATTER_ENDS = (256, 448, 640, 832, 1024)
-TURN_ON_SCALAR = (0, 3, 5, 7)
-HALVED = (0, 3, 4, 5)
-Y_ON_VECTOR = (0, 2, 3, 5, 6)
-LAG_SECOND = 2
+TURN_ON_SCALAR = (2, 4, 6, 7)
+HALVED = (1, 6)
+Y_ON_VECTOR = (1, 3)
+LAG_SECOND = 3
 LAG_TURN, LAG_QUANT, LAG_SCATTER = (1, 2, 2)
 
 
@@ -40,9 +40,9 @@ def tile_moe_two_mlp_silu_kernel(
     with ExitStack() as ctx:
         held = ctx.enter_context(tc.tile_pool(name="held", bufs=1))
         ring = ctx.enter_context(tc.tile_pool(name="ring", bufs=8))
-        psum_a = ctx.enter_context(tc.psum_pool(name="psum_a", bufs=5))
-        psum_t = ctx.enter_context(tc.psum_pool(name="psum_t", bufs=2))
-        psum_y = ctx.enter_context(tc.psum_pool(name="psum_y", bufs=1))
+        psum_a = ctx.enter_context(tc.psum_pool(name="psum_a", bufs=3))
+        psum_t = ctx.enter_context(tc.psum_pool(name="psum_t", bufs=3))
+        psum_y = ctx.enter_context(tc.psum_pool(name="psum_y", bufs=2))
 
         offs_sb = held.tile([P, SLOTS // 16], U16, name="offs_sb")
         dst_sb = held.tile([P, SLOTS // 16], U16, name="dst_sb")
@@ -62,9 +62,9 @@ def tile_moe_two_mlp_silu_kernel(
         ident = held.tile([P, P], F32, name="ident", align_bytes=64)
         zero = held.tile([P, 2], F32, name="zero")
 
-        def load_plane(queue, plane, rows):
+        def load_plane(queues, plane, rows):
             for r in range(4):
-                queue.dma_start(out=plane[r:P:32], in_=rows[r])
+                queues[r].dma_start(out=plane[r:P:32], in_=rows[r])
 
         def load_w1_words(queue, g):
             src = w1_words.bitcast(I32)[WORD_GROUPS[g][0]:WORD_GROUPS[g][-1] + 1, 0].rearrange("e p b -> p e b")
@@ -87,20 +87,19 @@ def tile_moe_two_mlp_silu_kernel(
         nc.sync.dma_start(offs_sb[:], offs)
         nc.scalar.activation(out=out_sb[:], in_=zero[:, 0:1].to_broadcast([P, T]), func=SILU)
         nc.sync.dma_start(dst_sb[:], dst)
-        load_plane(nc.sync, tok_scales[:].bitcast(I32), x_scales.bitcast(I32)[0].rearrange("(q r) t -> r q t", r=4))
+        load_plane((nc.sync, nc.sync, nc.sync, nc.sync), tok_scales[:].bitcast(I32), x_scales.bitcast(I32)[0].rearrange("(q r) t -> r q t", r=4))
         nc.sync.dma_start(out=tok_words[:], in_=x_words[0].rearrange("p t r -> p (t r)").bitcast(I32))
-        load_w1_words(nc.scalar, 0)
-        load_w1_scales(nc.sync, 0)
+        load_w1_words(nc.sync, 0)
+        load_w1_scales((nc.scalar, nc.scalar, nc.sync, nc.sync), 0)
         load_w1_words(nc.sync, 1)
         load_w1_words(nc.sync, 2)
-        load_w1_scales(nc.scalar, 1)
-        load_plane(nc.sync, w2s[:].bitcast(I32), w2_scales.bitcast(I32).rearrange("e s (q r) n -> r q (e s) n", r=4))
-        load_w2_words(nc.sync, 0, 4)
+        load_plane((nc.scalar, nc.sync, nc.sync, nc.sync), w2s[:].bitcast(I32), w2_scales.bitcast(I32).rearrange("e s (q r) n -> r q (e s) n", r=4))
+        load_w2_words(nc.sync, 0, 2)
+        load_w1_scales((nc.scalar, nc.scalar, nc.scalar, nc.scalar), 1)
+        nc.scalar.dma_start(out=gate_sb[:, 0:256], in_=gate[:, 0:256])
         load_w1_words(nc.sync, 3)
-        nc.sync.dma_start(out=gate_sb[:, 0:256], in_=gate[:, 0:256])
-        load_w1_words(nc.sync, 4)
+        load_w2_words(nc.sync, 2, 8)
         nc.sync.dma_start(out=gate_sb[:, 256:1024], in_=gate[:, 256:1024])
-        load_w2_words(nc.sync, 4, 8)
 
         def gather(lo, hi, sorts):
             picks = offs_sb[:, lo // 16:hi // 16]
@@ -184,14 +183,16 @@ def tile_moe_two_mlp_silu_kernel(
                     stop=(s == PASSES - 1),
                 )
             if e == group[-1]:
-                cols = slice(group[0] * C, (e + 1) * C)
-                nc.vector.tensor_tensor(y_sb[:, cols], y[:], gate_sb[:, cols], MULT)
+                if e in Y_ON_VECTOR:
+                    nc.vector.tensor_copy(out=y_sb[:, group[0] * C:(e + 1) * C], in_=y[:])
+                else:
+                    nc.scalar.copy(out=y_sb[:, group[0] * C:(e + 1) * C], in_=y[:])
                 return (e + 1) * C
             return group[0] * C
 
         def scatter(lo, hi):
             places = dst_sb[:, lo // 16:hi // 16]
-            nc.vector.tensor_copy(out_sb[:].indirect(places), y_sb[:, lo:hi])
+            nc.vector.tensor_tensor(out_sb[:].indirect(places), y_sb[:, lo:hi], gate_sb[:, lo:hi], MULT)
 
         scattered = 0
         done = 0

@@ -21,16 +21,16 @@ MULT = mybir.AluOpType.mult
 P = 128
 PASS = 512
 PASSES = H // PASS
-GATHERS = ((0, 192, 0, "bw"), (192, 512, 0, "bw"), (512, 1024, 2, "bw"))
-SCALE_GROUPS = ((0, 1, 2), (3, 4, 5, 6, 7))
+GATHERS = ((0, 256, 0, "bw"), (256, 512, 0, "bw"), (512, 768, 1, "bw"), (768, 1024, 2, "bw"))
+SCALE_GROUPS = ((0, 1), (2, 3, 4, 5, 6, 7))
 WORD_GROUPS = ((0,), (1, 2), (3, 4), (5, 6, 7))
 Y_GROUPS = ((0,), (1,), (2,), (3,), (4,), (5,), (6,), (7,))
-SCATTER_ENDS = (256, 448, 640, 832, 1024)
-TURN_ON_SCALAR = (2, 4, 6, 7)
-HALVED = (1, 6)
-Y_ON_VECTOR = (1, 3)
+SCATTER_ENDS = (256, 512, 768, 1024)
+TURN_ON_SCALAR = (0, 4, 6, 7)
+HALVED = (4, 7)
+Y_ON_VECTOR = (1, 2, 3)
 LAG_SECOND = 3
-LAG_TURN, LAG_QUANT, LAG_SCATTER = (1, 2, 2)
+LAG_TURN, LAG_QUANT, LAG_SCATTER = (1, 2, 1)
 
 
 def tile_moe_two_mlp_silu_kernel(
@@ -40,6 +40,7 @@ def tile_moe_two_mlp_silu_kernel(
     with ExitStack() as ctx:
         held = ctx.enter_context(tc.tile_pool(name="held", bufs=1))
         ring = ctx.enter_context(tc.tile_pool(name="ring", bufs=8))
+        picked = ctx.enter_context(tc.tile_pool(name="picked", bufs=3))
         psum_a = ctx.enter_context(tc.psum_pool(name="psum_a", bufs=3))
         psum_t = ctx.enter_context(tc.psum_pool(name="psum_t", bufs=3))
         psum_y = ctx.enter_context(tc.psum_pool(name="psum_y", bufs=2))
@@ -48,8 +49,6 @@ def tile_moe_two_mlp_silu_kernel(
         dst_sb = held.tile([P, SLOTS // 16], U16, name="dst_sb")
         tok_words = held.tile([P, T], I32, name="tok_words", align_bytes=64)
         tok_scales = held.tile([P, T], U8, name="tok_scales", align_bytes=64)
-        slot_words = held.tile([P, SLOTS], U32, name="slot_words", align_bytes=64)
-        slot_scales = held.tile([P, SLOTS], U8, name="slot_scales", align_bytes=64)
         w1w = [held.tile([P, len(grp), 2 * H], U8, name="w1w%d" % g, align_bytes=64) for g, grp in enumerate(WORD_GROUPS)]
         w1w_of = {e: w1w[g][:, e - grp[0], :] for g, grp in enumerate(WORD_GROUPS) for e in grp}
         w1s = [held.tile([P, len(grp), H], U8, name="w1s%d" % g, align_bytes=64) for g, grp in enumerate(SCALE_GROUPS)]
@@ -85,28 +84,33 @@ def tile_moe_two_mlp_silu_kernel(
         nc.vector.memset(w2s[:].bitcast(I32), 0)
         make_identity(nc, ident[:])
         nc.sync.dma_start(offs_sb[:], offs)
-        nc.scalar.activation(out=out_sb[:], in_=zero[:, 0:1].to_broadcast([P, T]), func=SILU)
-        nc.sync.dma_start(dst_sb[:], dst)
         load_plane((nc.sync, nc.sync, nc.sync, nc.sync), tok_scales[:].bitcast(I32), x_scales.bitcast(I32)[0].rearrange("(q r) t -> r q t", r=4))
+        nc.sync.dma_start(dst_sb[:], dst)
         nc.sync.dma_start(out=tok_words[:], in_=x_words[0].rearrange("p t r -> p (t r)").bitcast(I32))
-        load_w1_words(nc.sync, 0)
-        load_w1_scales((nc.scalar, nc.scalar, nc.sync, nc.sync), 0)
+        load_w1_scales((nc.sync, nc.sync, nc.scalar, nc.scalar), 0)
         load_w1_words(nc.sync, 1)
+        load_w1_scales((nc.sync, nc.scalar, nc.sync, nc.scalar), 1)
         load_w1_words(nc.sync, 2)
-        load_plane((nc.scalar, nc.sync, nc.sync, nc.sync), w2s[:].bitcast(I32), w2_scales.bitcast(I32).rearrange("e s (q r) n -> r q (e s) n", r=4))
         load_w2_words(nc.sync, 0, 2)
-        load_w1_scales((nc.scalar, nc.scalar, nc.scalar, nc.scalar), 1)
-        nc.scalar.dma_start(out=gate_sb[:, 0:256], in_=gate[:, 0:256])
+        load_plane((nc.sync, nc.scalar, nc.scalar, nc.scalar), w2s[:].bitcast(I32), w2_scales.bitcast(I32).rearrange("e s (q r) n -> r q (e s) n", r=4))
         load_w1_words(nc.sync, 3)
+        nc.scalar.activation(out=out_sb[:], in_=zero[:, 0:1].to_broadcast([P, T]), func=SILU)
+        nc.sync.dma_start(out=gate_sb[:, 0:256], in_=gate[:, 0:256])
+        load_w1_words(nc.scalar, 0)
         load_w2_words(nc.sync, 2, 8)
         nc.sync.dma_start(out=gate_sb[:, 256:1024], in_=gate[:, 256:1024])
 
+        slots_of = {}
+
         def gather(lo, hi, sorts):
             picks = offs_sb[:, lo // 16:hi // 16]
-            if "b" in sorts:
-                nc.vector.tensor_copy(slot_scales[:, lo:hi], tok_scales[:].indirect(picks))
-            if "w" in sorts:
-                nc.vector.tensor_copy(slot_words[:, lo:hi], tok_words[:].bitcast(U32).indirect(picks))
+            slot_scales = picked.tile([P, hi - lo], U8, name="slot_scales", align_bytes=64)
+            slot_words = picked.tile([P, hi - lo], U32, name="slot_words", align_bytes=64)
+            nc.vector.tensor_copy(slot_scales[:], tok_scales[:].indirect(picks))
+            nc.vector.tensor_copy(slot_words[:], tok_words[:].bitcast(U32).indirect(picks))
+            for e in range(lo // C, hi // C):
+                cols = slice(e * C - lo, (e + 1) * C - lo)
+                slots_of[e] = (slot_words[:, cols], slot_scales[:, cols])
 
         h_of = {}
         grouped_of = {}
@@ -114,14 +118,13 @@ def tile_moe_two_mlp_silu_kernel(
         y_of = {}
 
         def first_layer(e):
-            cols = slice(e * C, (e + 1) * C)
             h = ring.tile([P, H], BF16, name="h", align_bytes=64)
             for s in range(PASSES):
                 a = psum_a.tile([P, PASS], F32, name="a")
                 nc.tensor.matmul_mx(
                     out=a[:],
-                    lhsT=slot_words[:, cols].bitcast(FP8X4),
-                    lhsT_scale=slot_scales[:, cols],
+                    lhsT=slots_of[e][0].bitcast(FP8X4),
+                    lhsT_scale=slots_of[e][1],
                     rhs=w1w_of[e][:, 2 * s * PASS:2 * (s + 1) * PASS].bitcast(FP4X4),
                     rhs_scale=w1s_of[e][:, s * PASS:(s + 1) * PASS],
                     start=True,

@@ -21,38 +21,41 @@ MULT = mybir.AluOpType.mult
 P = 128
 PASS = 512
 PASSES = H // PASS
-GATHERS = ((0, 256, 0, "bw"), (256, 512, 0, "bw"), (512, 768, 1, "bw"), (768, 1024, 2, "bw"))
-SCALE_GROUPS = ((0, 1), (2, 3, 4, 5, 6, 7))
-WORD_GROUPS = ((0,), (1, 2), (3, 4), (5, 6, 7))
-Y_GROUPS = ((0,), (1,), (2,), (3,), (4,), (5,), (6,), (7,))
-SCATTER_ENDS = (256, 512, 768, 1024)
-TURN_ON_SCALAR = (0, 4, 6, 7)
-HALVED = (4, 7)
-Y_ON_VECTOR = (1, 2, 3)
-LAG_SECOND = 3
-LAG_TURN, LAG_QUANT, LAG_SCATTER = (1, 2, 1)
+STRIPE = 16
+QUADRANT = 32
+ROWS = 4
+
+GATHERS = ((range(0, 2), 0), (range(2, 6), 0), (range(6, 8), 2))
+W1_PLANES = (range(0, 2), range(2, 8))
+W2_FIRST = 4
+GATE_FIRST = 2 * C
+Y_GROUPS = (range(0, 2), range(2, 4), range(4, 5), range(5, 6), range(6, 7), range(7, 8))
+TURNED_ON_SCALAR = (0, 4, 6, 7)
+FIRST_Y_ON_SCALAR = 4
+SCATTER = 2 * C
+LAG_TURN, LAG_QUANTISE, LAG_SECOND, LAG_SCATTER = 1, 2, 3, 1
 
 
 def tile_moe_two_mlp_silu_kernel(
     tc, x_words, x_scales, w1_words, w1_scales, w2_words, w2_scales, gate, offs, dst, out
 ):
     nc = tc.nc
+    sync, scalar, gpsimd = nc.sync, nc.scalar, nc.gpsimd
     with ExitStack() as ctx:
         held = ctx.enter_context(tc.tile_pool(name="held", bufs=1))
-        ring = ctx.enter_context(tc.tile_pool(name="ring", bufs=8))
-        picked = ctx.enter_context(tc.tile_pool(name="picked", bufs=3))
+        per_expert = ctx.enter_context(tc.tile_pool(name="per_expert", bufs=E))
+        picked = ctx.enter_context(tc.tile_pool(name="picked", bufs=2))
         psum_a = ctx.enter_context(tc.psum_pool(name="psum_a", bufs=3))
         psum_t = ctx.enter_context(tc.psum_pool(name="psum_t", bufs=3))
         psum_y = ctx.enter_context(tc.psum_pool(name="psum_y", bufs=2))
 
-        offs_sb = held.tile([P, SLOTS // 16], U16, name="offs_sb")
-        dst_sb = held.tile([P, SLOTS // 16], U16, name="dst_sb")
+        offs_sb = held.tile([P, SLOTS // STRIPE], U16, name="offs_sb")
+        dst_sb = held.tile([P, SLOTS // STRIPE], U16, name="dst_sb")
         tok_words = held.tile([P, T], I32, name="tok_words", align_bytes=64)
         tok_scales = held.tile([P, T], U8, name="tok_scales", align_bytes=64)
-        w1w = [held.tile([P, len(grp), 2 * H], U8, name="w1w%d" % g, align_bytes=64) for g, grp in enumerate(WORD_GROUPS)]
-        w1w_of = {e: w1w[g][:, e - grp[0], :] for g, grp in enumerate(WORD_GROUPS) for e in grp}
-        w1s = [held.tile([P, len(grp), H], U8, name="w1s%d" % g, align_bytes=64) for g, grp in enumerate(SCALE_GROUPS)]
-        w1s_of = {e: w1s[g][:, e - grp[0], :] for g, grp in enumerate(SCALE_GROUPS) for e in grp}
+        w1w = [held.tile([P, 2 * H], U8, name="w1w%d" % e, align_bytes=64) for e in range(E)]
+        w1s = [held.tile([P, len(grp), H], U8, name="w1s%d" % g, align_bytes=64) for g, grp in enumerate(W1_PLANES)]
+        w1s_of = {e: w1s[g][:, e - grp.start, :] for g, grp in enumerate(W1_PLANES) for e in grp}
         w2w = held.tile([P, E * PASSES, 2 * N], U8, name="w2w", align_bytes=64)
         w2s = held.tile([P, E * PASSES, N], U8, name="w2s", align_bytes=64)
         gate_sb = held.tile([P, SLOTS], F32, name="gate_sb")
@@ -62,70 +65,75 @@ def tile_moe_two_mlp_silu_kernel(
         zero = held.tile([P, 2], F32, name="zero")
 
         def load_plane(queues, plane, rows):
-            for r in range(4):
-                queues[r].dma_start(out=plane[r:P:32], in_=rows[r])
+            for r in range(ROWS):
+                queues[r].dma_start(out=plane[:].bitcast(I32)[r:P:QUADRANT], in_=rows[r])
 
-        def load_w1_words(queue, g):
-            src = w1_words.bitcast(I32)[WORD_GROUPS[g][0]:WORD_GROUPS[g][-1] + 1, 0].rearrange("e p b -> p e b")
-            queue.dma_start(out=w1w[g][:].bitcast(I32), in_=src)
+        def load_w1_scales(queues, g):
+            src = w1_scales.bitcast(I32)[W1_PLANES[g].start:W1_PLANES[g].stop, 0]
+            load_plane(queues, w1s[g], src.rearrange("e (q r) i -> r q e i", r=ROWS))
 
-        def load_w1_scales(queue, g):
-            src = w1_scales.bitcast(I32)[SCALE_GROUPS[g][0]:SCALE_GROUPS[g][-1] + 1, 0]
-            load_plane(queue, w1s[g][:].bitcast(I32), src.rearrange("e (q r) i -> r q e i", r=4))
+        def load_w1_words(queue, e):
+            queue.dma_start(out=w1w[e][:].bitcast(I32), in_=w1_words.bitcast(I32)[e, 0])
 
-        def load_w2_words(queue, lo, hi):
+        def load_w2_words(lo, hi):
             src = w2_words.bitcast(I32)[lo:hi].rearrange("e s p b -> p (e s) b")
-            queue.dma_start(out=w2w[:, lo * PASSES:hi * PASSES, :].bitcast(I32), in_=src)
+            sync.dma_start(out=w2w[:, lo * PASSES:hi * PASSES, :].bitcast(I32), in_=src)
+
+        def load_gate(lo, hi):
+            sync.dma_start(out=gate_sb[:, lo:hi], in_=gate[:, lo:hi])
 
         nc.vector.memset(tok_scales[:].bitcast(I32), 0)
         nc.vector.memset(zero[:], 0.0)
-        nc.vector.memset(w1s[0][:].bitcast(I32), 0)
-        nc.vector.memset(w1s[1][:].bitcast(I32), 0)
-        nc.vector.memset(w2s[:].bitcast(I32), 0)
+        for plane in (w1s[0], w1s[1], w2s):
+            nc.vector.memset(plane[:].bitcast(I32), 0)
         make_identity(nc, ident[:])
-        nc.sync.dma_start(offs_sb[:], offs)
-        load_plane((nc.sync, nc.sync, nc.sync, nc.sync), tok_scales[:].bitcast(I32), x_scales.bitcast(I32)[0].rearrange("(q r) t -> r q t", r=4))
-        nc.sync.dma_start(dst_sb[:], dst)
-        nc.sync.dma_start(out=tok_words[:], in_=x_words[0].rearrange("p t r -> p (t r)").bitcast(I32))
-        load_w1_scales((nc.sync, nc.sync, nc.scalar, nc.scalar), 0)
-        load_w1_words(nc.sync, 1)
-        load_w1_scales((nc.sync, nc.scalar, nc.sync, nc.scalar), 1)
-        load_w1_words(nc.sync, 2)
-        load_w2_words(nc.sync, 0, 2)
-        load_plane((nc.sync, nc.scalar, nc.scalar, nc.scalar), w2s[:].bitcast(I32), w2_scales.bitcast(I32).rearrange("e s (q r) n -> r q (e s) n", r=4))
-        load_w1_words(nc.sync, 3)
+
+        sync.dma_start(offs_sb[:], offs)
+        sync.dma_start(dst_sb[:], dst)
+        load_plane([sync] * ROWS, tok_scales, x_scales.bitcast(I32)[0].rearrange("(q r) t -> r q t", r=ROWS))
+        sync.dma_start(out=tok_words[:], in_=x_words[0].rearrange("p t r -> p (t r)").bitcast(I32))
+        load_w1_words(scalar, 0)
+        load_w1_scales([gpsimd, sync, sync, sync], 0)
         nc.scalar.activation(out=out_sb[:], in_=zero[:, 0:1].to_broadcast([P, T]), func=SILU)
-        nc.sync.dma_start(out=gate_sb[:, 0:256], in_=gate[:, 0:256])
-        load_w1_words(nc.scalar, 0)
-        load_w2_words(nc.sync, 2, 8)
-        nc.sync.dma_start(out=gate_sb[:, 256:1024], in_=gate[:, 256:1024])
+        load_w1_words(sync, 1)
+        load_w1_scales([sync, sync, scalar, scalar], 1)
+        load_w1_words(sync, 2)
+        load_gate(0, GATE_FIRST)
+        for e in (3, 4, 5):
+            load_w1_words(sync, e)
+        load_w2_words(0, W2_FIRST)
+        for e in (6, 7):
+            load_w1_words(sync, e)
+        load_gate(GATE_FIRST, SLOTS)
+        load_plane([scalar] * ROWS, w2s, w2_scales.bitcast(I32).rearrange("e s (q r) n -> r q (e s) n", r=ROWS))
+        load_w2_words(W2_FIRST, E)
 
         slots_of = {}
+        h_of = {}
+        grouped_of = {}
+        codes_of = {}
 
-        def gather(lo, hi, sorts):
-            picks = offs_sb[:, lo // 16:hi // 16]
+        def gather(experts):
+            lo, hi = experts.start * C, experts.stop * C
+            picks = offs_sb[:, lo // STRIPE:hi // STRIPE]
             slot_scales = picked.tile([P, hi - lo], U8, name="slot_scales", align_bytes=64)
             slot_words = picked.tile([P, hi - lo], U32, name="slot_words", align_bytes=64)
             nc.vector.tensor_copy(slot_scales[:], tok_scales[:].indirect(picks))
             nc.vector.tensor_copy(slot_words[:], tok_words[:].bitcast(U32).indirect(picks))
-            for e in range(lo // C, hi // C):
+            for e in experts:
                 cols = slice(e * C - lo, (e + 1) * C - lo)
                 slots_of[e] = (slot_words[:, cols], slot_scales[:, cols])
 
-        h_of = {}
-        grouped_of = {}
-        codes_of = {}
-        y_of = {}
-
         def first_layer(e):
-            h = ring.tile([P, H], BF16, name="h", align_bytes=64)
+            slot_words, slot_scales = slots_of[e]
+            h = per_expert.tile([P, H], BF16, name="h", align_bytes=64)
             for s in range(PASSES):
                 a = psum_a.tile([P, PASS], F32, name="a")
                 nc.tensor.matmul_mx(
                     out=a[:],
-                    lhsT=slots_of[e][0].bitcast(FP8X4),
-                    lhsT_scale=slots_of[e][1],
-                    rhs=w1w_of[e][:, 2 * s * PASS:2 * (s + 1) * PASS].bitcast(FP4X4),
+                    lhsT=slot_words.bitcast(FP8X4),
+                    lhsT_scale=slot_scales,
+                    rhs=w1w[e][:, 2 * s * PASS:2 * (s + 1) * PASS].bitcast(FP4X4),
                     rhs_scale=w1s_of[e][:, s * PASS:(s + 1) * PASS],
                     start=True,
                     stop=True,
@@ -138,85 +146,80 @@ def tile_moe_two_mlp_silu_kernel(
             h_of[e] = h
 
         def pieces(e):
-            return [(0,), (1,)] if e in HALVED else [(0, 1)]
+            return [range(s, s + 1) for s in range(PASSES)] if e == E - 1 else [range(PASSES)]
 
         def turn(e):
             pairs = h_of[e][:].bitcast(F32)
-            grouped = ring.tile([P, PASSES * C * 4], BF16, name="grouped", align_bytes=64)
+            grouped = per_expert.tile([P, PASSES * C * 4], BF16, name="grouped", align_bytes=64)
             for piece in pieces(e):
                 turned = psum_t.tile([P, len(piece), 2, C], F32, name="turned")
                 for s in piece:
                     for u in range(2):
-                        b = 2 * s + u
-                        nc.tensor.transpose(turned[:, s - piece[0], u, :], pairs[:, b * P:(b + 1) * P], ident[:])
-                words = grouped[:].bitcast(F32)[:, piece[0] * 2 * C:(piece[-1] + 1) * 2 * C]
-                to = words.rearrange("p (s c u) -> p s c u", s=len(piece), u=2)
-                frm = turned[:].rearrange("p s u c -> p s c u")
-                if e in TURN_ON_SCALAR:
-                    nc.scalar.copy(out=to, in_=frm)
+                        first = (2 * s + u) * P
+                        nc.tensor.transpose(turned[:, s - piece.start, u, :], pairs[:, first:first + P], ident[:])
+                words = grouped[:].bitcast(F32)[:, piece.start * 2 * C:piece.stop * 2 * C]
+                side_by_side = words.rearrange("p (s c u) -> p s c u", s=len(piece), u=2)
+                apart = turned[:].rearrange("p s u c -> p s c u")
+                if e in TURNED_ON_SCALAR:
+                    nc.scalar.copy(out=side_by_side, in_=apart)
                 else:
-                    nc.vector.tensor_copy(out=to, in_=frm)
+                    nc.vector.tensor_copy(out=side_by_side, in_=apart)
             grouped_of[e] = grouped
 
         def quantise(e):
-            codes = ring.tile([P, PASSES * C], U32, name="codes", align_bytes=64)
-            scales = ring.tile([P, PASSES * C], U8, name="scales", align_bytes=64)
+            codes = per_expert.tile([P, PASSES * C], U32, name="codes", align_bytes=64)
+            scales = per_expert.tile([P, PASSES * C], U8, name="scales", align_bytes=64)
             for piece in pieces(e):
-                lo, hi = piece[0] * C, (piece[-1] + 1) * C
+                lo, hi = piece.start * C, piece.stop * C
                 nc.vector.quantize_mx(
                     out=codes[:, lo:hi].bitcast(FP8X4), scales=scales[:, lo:hi], in_=grouped_of[e][:, 4 * lo:4 * hi]
                 )
             codes_of[e] = (codes, scales)
 
-        def second_layer(e):
-            codes, scales = codes_of[e]
-            group = [grp for grp in Y_GROUPS if e in grp][0]
-            if e == group[0]:
-                y_of[group] = psum_y.tile([P, len(group) * C], F32, name="y")
-            y = y_of[group]
-            place = (e - group[0]) * C
-            for s in range(PASSES):
-                nc.tensor.matmul_mx(
-                    out=y[:, place:place + C],
-                    lhsT=w2w[:, e * PASSES + s, :].bitcast(FP4X4),
-                    lhsT_scale=w2s[:, e * PASSES + s, :],
-                    rhs=codes[:, s * C:(s + 1) * C].bitcast(FP8X4),
-                    rhs_scale=scales[:, s * C:(s + 1) * C],
-                    start=(s == 0),
-                    stop=(s == PASSES - 1),
-                )
-            if e == group[-1]:
-                if e in Y_ON_VECTOR:
-                    nc.vector.tensor_copy(out=y_sb[:, group[0] * C:(e + 1) * C], in_=y[:])
-                else:
-                    nc.scalar.copy(out=y_sb[:, group[0] * C:(e + 1) * C], in_=y[:])
-                return (e + 1) * C
-            return group[0] * C
+        def second_layer(experts):
+            y = psum_y.tile([P, len(experts) * C], F32, name="y")
+            for e in experts:
+                codes, scales = codes_of[e]
+                place = (e - experts.start) * C
+                for s in range(PASSES):
+                    nc.tensor.matmul_mx(
+                        out=y[:, place:place + C],
+                        lhsT=w2w[:, e * PASSES + s, :].bitcast(FP4X4),
+                        lhsT_scale=w2s[:, e * PASSES + s, :],
+                        rhs=codes[:, s * C:(s + 1) * C].bitcast(FP8X4),
+                        rhs_scale=scales[:, s * C:(s + 1) * C],
+                        start=(s == 0),
+                        stop=(s == PASSES - 1),
+                    )
+            cols = slice(experts.start * C, experts.stop * C)
+            if experts.start < FIRST_Y_ON_SCALAR:
+                nc.vector.tensor_tensor(y_sb[:, cols], y[:], gate_sb[:, cols], MULT)
+            else:
+                nc.scalar.copy(out=y_sb[:, cols], in_=y[:])
 
-        def scatter(lo, hi):
-            places = dst_sb[:, lo // 16:hi // 16]
-            nc.vector.tensor_tensor(out_sb[:].indirect(places), y_sb[:, lo:hi], gate_sb[:, lo:hi], MULT)
+        def scatter(lo):
+            hi = lo + SCATTER
+            places = dst_sb[:, lo // STRIPE:hi // STRIPE]
+            if lo < FIRST_Y_ON_SCALAR * C:
+                nc.vector.tensor_copy(out_sb[:].indirect(places), y_sb[:, lo:hi])
+            else:
+                nc.vector.tensor_tensor(out_sb[:].indirect(places), y_sb[:, lo:hi], gate_sb[:, lo:hi], MULT)
 
-        scattered = 0
-        done = 0
-        done_at = {}
         for step in range(E + LAG_SECOND + LAG_SCATTER):
-            for lo, hi, at, sorts in GATHERS:
+            for experts, at in GATHERS:
                 if at == step:
-                    gather(lo, hi, sorts)
+                    gather(experts)
             if step < E:
                 first_layer(step)
             if 0 <= step - LAG_TURN < E:
                 turn(step - LAG_TURN)
-            if 0 <= step - LAG_QUANT < E:
-                quantise(step - LAG_QUANT)
-            if 0 <= step - LAG_SECOND < E:
-                done = second_layer(step - LAG_SECOND)
-            done_at[step] = done
-            for end in SCATTER_ENDS:
-                if scattered < end <= done_at.get(step - LAG_SCATTER, 0):
-                    scatter(scattered, end)
-                    scattered = end
-        assert scattered == SLOTS
+            if 0 <= step - LAG_QUANTISE < E:
+                quantise(step - LAG_QUANTISE)
+            for experts in Y_GROUPS:
+                if experts[-1] + LAG_SECOND == step:
+                    second_layer(experts)
+            for lo in range(0, SLOTS, SCATTER):
+                if (lo + SCATTER) // C - 1 + LAG_SECOND + LAG_SCATTER == step:
+                    scatter(lo)
 
-        nc.sync.dma_start(out=out[:, 0:1536], in_=out_sb[:, 0:1536])
+        sync.dma_start(out=out, in_=out_sb[:])

@@ -64,13 +64,16 @@ def tile_moe_two_mlp_silu_kernel(
         ident = held.tile([P, P], F32, name="ident", align_bytes=64)
         zero = held.tile([P, 2], F32, name="zero")
 
-        def load_plane(queues, plane, rows):
-            for r in range(ROWS):
-                queues[r].dma_start(out=plane[:].bitcast(I32)[r:P:QUADRANT], in_=rows[r])
+        def load_rows(queue, plane, rows, which):
+            for r in which:
+                queue.dma_start(out=plane[:].bitcast(I32)[r:P:QUADRANT], in_=rows[r])
 
-        def load_w1_scales(queues, g):
-            src = w1_scales.bitcast(I32)[W1_PLANES[g].start:W1_PLANES[g].stop, 0]
-            load_plane(queues, w1s[g], src.rearrange("e (q r) i -> r q e i", r=ROWS))
+        x_rows = x_scales.bitcast(I32)[0].rearrange("(q r) t -> r q t", r=ROWS)
+        w2_rows = w2_scales.bitcast(I32).rearrange("e s (q r) n -> r q (e s) n", r=ROWS)
+        w1_rows = [
+            w1_scales.bitcast(I32)[group.start:group.stop, 0].rearrange("e (q r) i -> r q e i", r=ROWS)
+            for group in W1_PLANES
+        ]
 
         def load_w1_words(queue, e):
             queue.dma_start(out=w1w[e][:].bitcast(I32), in_=w1_words.bitcast(I32)[e, 0])
@@ -84,29 +87,33 @@ def tile_moe_two_mlp_silu_kernel(
 
         nc.vector.memset(tok_scales[:].bitcast(I32), 0)
         nc.vector.memset(zero[:], 0.0)
-        for plane in (w1s[0], w1s[1], w2s):
+        for plane in (w1s[0], w2s, w1s[1]):
             nc.vector.memset(plane[:].bitcast(I32), 0)
         make_identity(nc, ident[:])
 
         sync.dma_start(offs_sb[:], offs)
         sync.dma_start(dst_sb[:], dst)
-        load_plane([sync] * ROWS, tok_scales, x_scales.bitcast(I32)[0].rearrange("(q r) t -> r q t", r=ROWS))
+        load_rows(sync, tok_scales, x_rows, (0, 1, 2, 3,))
         sync.dma_start(out=tok_words[:], in_=x_words[0].rearrange("p t r -> p (t r)").bitcast(I32))
         load_w1_words(scalar, 0)
-        load_w1_scales([gpsimd, sync, sync, sync], 0)
+        load_rows(gpsimd, w1s[0], w1_rows[0], (0,))
+        load_rows(sync, w1s[0], w1_rows[0], (1, 2, 3,))
         nc.scalar.activation(out=out_sb[:], in_=zero[:, 0:1].to_broadcast([P, T]), func=SILU)
         load_w1_words(sync, 1)
-        load_w1_scales([sync, sync, scalar, scalar], 1)
+        load_rows(scalar, w2s, w2_rows, (0, 1,))
+        load_rows(sync, w1s[1], w1_rows[1], (0, 1,))
+        load_rows(scalar, w1s[1], w1_rows[1], (2, 3,))
+        load_rows(scalar, w2s, w2_rows, (2, 3,))
         load_w1_words(sync, 2)
-        load_gate(0, GATE_FIRST)
-        for e in (3, 4, 5):
-            load_w1_words(sync, e)
-        load_w2_words(0, W2_FIRST)
-        for e in (6, 7):
-            load_w1_words(sync, e)
-        load_gate(GATE_FIRST, SLOTS)
-        load_plane([scalar] * ROWS, w2s, w2_scales.bitcast(I32).rearrange("e s (q r) n -> r q (e s) n", r=ROWS))
-        load_w2_words(W2_FIRST, E)
+        load_gate(0 * C, 2 * C)
+        load_w1_words(sync, 3)
+        load_w1_words(sync, 4)
+        load_w1_words(sync, 5)
+        load_w2_words(0, 4)
+        load_w1_words(sync, 6)
+        load_w1_words(sync, 7)
+        load_gate(2 * C, 8 * C)
+        load_w2_words(4, 8)
 
         slots_of = {}
         h_of = {}

@@ -97,8 +97,9 @@ def tile_moe_two_mlp_silu_kernel(
         sync.dma_start(out=tok_words[:], in_=x_words[0].rearrange("p t r -> p (t r)").bitcast(I32))
         load_w1_words(scalar, 0)
         load_rows(gpsimd, w1s[0], w1_rows[0], (0,))
-        load_rows(sync, w1s[0], w1_rows[0], (1, 2, 3,))
+        load_rows(sync, w1s[0], w1_rows[0], (1, 2,))
         nc.scalar.activation(out=out_sb[:], in_=zero[:, 0:1].to_broadcast([P, T]), func=SILU)
+        load_rows(scalar, w1s[0], w1_rows[0], (3,))
         load_w1_words(sync, 1)
         load_rows(scalar, w2s, w2_rows, (0, 1,))
         load_rows(sync, w1s[1], w1_rows[1], (0, 1,))

@@ -25,7 +25,8 @@ STRIPE = 16
 QUADRANT = 32
 ROWS = 4
 
-GATHERS = ((range(0, 2), 0), (range(2, 6), 0), (range(6, 8), 2))
+SCALE_GATHERS = ((range(0, 2), 0), (range(2, 4), 0), (range(4, 8), 2))
+WORD_GATHERS = (range(0, 2), range(2, 8))
 W1_PLANES = (range(0, 2), range(2, 8))
 W2_FIRST = 4
 GATE_FIRST = 2 * C
@@ -93,9 +94,10 @@ def tile_moe_two_mlp_silu_kernel(
 
         sync.dma_start(offs_sb[:], offs)
         sync.dma_start(dst_sb[:], dst)
-        load_rows(sync, tok_scales, x_rows, (0, 1, 2, 3,))
-        sync.dma_start(out=tok_words[:], in_=x_words[0].rearrange("p t r -> p (t r)").bitcast(I32))
         load_w1_words(scalar, 0)
+        load_rows(scalar, tok_scales, x_rows, (0, 1,))
+        load_rows(sync, tok_scales, x_rows, (2, 3,))
+        sync.dma_start(out=tok_words[:], in_=x_words[0].rearrange("p t r -> p (t r)").bitcast(I32))
         load_rows(gpsimd, w1s[0], w1_rows[0], (0,))
         load_rows(sync, w1s[0], w1_rows[0], (1, 2,))
         nc.scalar.activation(out=out_sb[:], in_=zero[:, 0:1].to_broadcast([P, T]), func=SILU)
@@ -104,11 +106,12 @@ def tile_moe_two_mlp_silu_kernel(
         load_rows(scalar, w2s, w2_rows, (0, 1,))
         load_rows(sync, w1s[1], w1_rows[1], (0, 1,))
         load_rows(scalar, w1s[1], w1_rows[1], (2, 3,))
-        load_rows(scalar, w2s, w2_rows, (2, 3,))
+        load_rows(scalar, w2s, w2_rows, (2,))
         load_w1_words(sync, 2)
-        load_gate(0 * C, 2 * C)
         load_w1_words(sync, 3)
+        load_gate(0 * C, 2 * C)
         load_w1_words(sync, 4)
+        load_rows(sync, w2s, w2_rows, (3,))
         load_w1_words(sync, 5)
         load_w2_words(0, 4)
         load_w1_words(sync, 6)
@@ -116,31 +119,33 @@ def tile_moe_two_mlp_silu_kernel(
         load_gate(2 * C, 8 * C)
         load_w2_words(4, 8)
 
-        slots_of = {}
+        slot_words = held.tile([P, SLOTS], U32, name="slot_words", align_bytes=64)
+        scales_of = {}
         h_of = {}
         grouped_of = {}
         codes_of = {}
 
-        def gather(experts):
-            lo, hi = experts.start * C, experts.stop * C
-            picks = offs_sb[:, lo // STRIPE:hi // STRIPE]
-            slot_scales = picked.tile([P, hi - lo], U8, name="slot_scales", align_bytes=64)
-            slot_words = picked.tile([P, hi - lo], U32, name="slot_words", align_bytes=64)
-            nc.vector.tensor_copy(slot_scales[:], tok_scales[:].indirect(picks))
-            nc.vector.tensor_copy(slot_words[:], tok_words[:].bitcast(U32).indirect(picks))
+        def picks(experts):
+            return offs_sb[:, experts.start * C // STRIPE:experts.stop * C // STRIPE]
+
+        def gather_scales(experts):
+            slot_scales = picked.tile([P, len(experts) * C], U8, name="slot_scales", align_bytes=64)
+            nc.vector.tensor_copy(slot_scales[:], tok_scales[:].indirect(picks(experts)))
             for e in experts:
-                cols = slice(e * C - lo, (e + 1) * C - lo)
-                slots_of[e] = (slot_words[:, cols], slot_scales[:, cols])
+                scales_of[e] = slot_scales[:, (e - experts.start) * C:(e - experts.start + 1) * C]
+
+        def gather_words(experts):
+            cols = slice(experts.start * C, experts.stop * C)
+            nc.vector.tensor_copy(slot_words[:, cols], tok_words[:].bitcast(U32).indirect(picks(experts)))
 
         def first_layer(e):
-            slot_words, slot_scales = slots_of[e]
             h = per_expert.tile([P, H], BF16, name="h", align_bytes=64)
             for s in range(PASSES):
                 a = psum_a.tile([P, PASS], F32, name="a")
                 nc.tensor.matmul_mx(
                     out=a[:],
-                    lhsT=slot_words.bitcast(FP8X4),
-                    lhsT_scale=slot_scales,
+                    lhsT=slot_words[:, e * C:(e + 1) * C].bitcast(FP8X4),
+                    lhsT_scale=scales_of[e],
                     rhs=w1w[e][:, 2 * s * PASS:2 * (s + 1) * PASS].bitcast(FP4X4),
                     rhs_scale=w1s_of[e][:, s * PASS:(s + 1) * PASS],
                     start=True,
@@ -214,9 +219,12 @@ def tile_moe_two_mlp_silu_kernel(
                 nc.vector.tensor_tensor(out_sb[:].indirect(places), y_sb[:, lo:hi], gate_sb[:, lo:hi], MULT)
 
         for step in range(E + LAG_SECOND + LAG_SCATTER):
-            for experts, at in GATHERS:
+            for experts, at in SCALE_GATHERS:
                 if at == step:
-                    gather(experts)
+                    gather_scales(experts)
+            if step == 0:
+                for experts in WORD_GATHERS:
+                    gather_words(experts)
             if step < E:
                 first_layer(step)
             if 0 <= step - LAG_TURN < E:

@@ -99,9 +99,8 @@ def tile_moe_two_mlp_silu_kernel(
         load_rows(sync, tok_scales, x_rows, (2, 3,))
         sync.dma_start(out=tok_words[:], in_=x_words[0].rearrange("p t r -> p (t r)").bitcast(I32))
         load_rows(gpsimd, w1s[0], w1_rows[0], (0,))
-        load_rows(sync, w1s[0], w1_rows[0], (1, 2,))
+        load_rows(sync, w1s[0], w1_rows[0], (1, 2, 3,))
         nc.scalar.activation(out=out_sb[:], in_=zero[:, 0:1].to_broadcast([P, T]), func=SILU)
-        load_rows(scalar, w1s[0], w1_rows[0], (3,))
         load_w1_words(sync, 1)
         load_rows(scalar, w2s, w2_rows, (0, 1,))
         load_rows(sync, w1s[1], w1_rows[1], (0, 1,))
@@ -109,11 +108,11 @@ def tile_moe_two_mlp_silu_kernel(
         load_rows(scalar, w2s, w2_rows, (2,))
         load_w1_words(sync, 2)
         load_w1_words(sync, 3)
-        load_gate(0 * C, 2 * C)
         load_w1_words(sync, 4)
-        load_rows(sync, w2s, w2_rows, (3,))
         load_w1_words(sync, 5)
+        load_rows(sync, w2s, w2_rows, (3,))
         load_w2_words(0, 4)
+        load_gate(0 * C, 2 * C)
         load_w1_words(sync, 6)
         load_w1_words(sync, 7)
         load_gate(2 * C, 8 * C)

@@ -27,7 +27,7 @@ ROWS = 4
 
 SCALE_GATHERS = ((range(0, 2), 0), (range(2, 4), 0), (range(4, 8), 2))
 WORD_GATHERS = (range(0, 2), range(2, 8))
-W1_PLANES = (range(0, 2), range(2, 8))
+W1_PLANES = (range(0, 3), range(3, 8))
 W2_FIRST = 4
 GATE_FIRST = 2 * C
 Y_GROUPS = (range(0, 2), range(2, 4), range(4, 5), range(5, 6), range(6, 7), range(7, 8))
@@ -98,19 +98,20 @@ def tile_moe_two_mlp_silu_kernel(
         load_rows(scalar, tok_scales, x_rows, (0, 1,))
         load_rows(sync, tok_scales, x_rows, (2, 3,))
         sync.dma_start(out=tok_words[:], in_=x_words[0].rearrange("p t r -> p (t r)").bitcast(I32))
-        load_rows(gpsimd, w1s[0], w1_rows[0], (0,))
-        load_rows(sync, w1s[0], w1_rows[0], (1, 2, 3,))
+        load_rows(sync, w1s[0], w1_rows[0], (0, 1,))
         nc.scalar.activation(out=out_sb[:], in_=zero[:, 0:1].to_broadcast([P, T]), func=SILU)
+        load_rows(scalar, w1s[0], w1_rows[0], (2, 3,))
+        load_rows(gpsimd, w2s, w2_rows, (0,))
         load_w1_words(sync, 1)
-        load_rows(scalar, w2s, w2_rows, (0, 1,))
+        load_w1_words(sync, 2)
+        load_rows(scalar, w2s, w2_rows, (1,))
         load_rows(sync, w1s[1], w1_rows[1], (0, 1,))
         load_rows(scalar, w1s[1], w1_rows[1], (2, 3,))
         load_rows(scalar, w2s, w2_rows, (2,))
-        load_w1_words(sync, 2)
+        load_rows(sync, w2s, w2_rows, (3,))
         load_w1_words(sync, 3)
         load_w1_words(sync, 4)
         load_w1_words(sync, 5)
-        load_rows(sync, w2s, w2_rows, (3,))
         load_w2_words(0, 4)
         load_gate(0 * C, 2 * C)
         load_w1_words(sync, 6)

@@ -25,16 +25,12 @@ STRIPE = 16
 QUADRANT = 32
 ROWS = 4
 
-SCALE_GATHERS = ((range(0, 2), 0), (range(2, 4), 0), (range(4, 8), 2))
-WORD_GATHERS = (range(0, 2), range(2, 8))
-W1_PLANES = (range(0, 3), range(3, 8))
-W2_FIRST = 4
-GATE_FIRST = 2 * C
-Y_GROUPS = (range(0, 2), range(2, 4), range(4, 5), range(5, 6), range(6, 7), range(7, 8))
-TURNED_ON_SCALAR = (0, 4, 6, 7)
-FIRST_Y_ON_SCALAR = 4
-SCATTER = 2 * C
-LAG_TURN, LAG_QUANTISE, LAG_SECOND, LAG_SCATTER = 1, 2, 3, 1
+W1_PLANES = (range(0, 3), range(3, 8),)
+W1_LOADS = (range(0, 1), range(1, 2), range(2, 3), range(3, 4), range(4, 5), range(5, 6), range(6, 7), range(7, 8),)
+QUANTISED = (range(0, 1), range(1, 2), range(2, 3), range(3, 4), range(4, 5), range(5, 6), range(6, 7), range(7, 8),)
+FIRST_SCALES = 384
+BANK = 2048
+WARM_PASSES, WARM_COLUMNS = 5, 256
 
 
 def tile_moe_two_mlp_silu_kernel(
@@ -44,17 +40,14 @@ def tile_moe_two_mlp_silu_kernel(
     sync, scalar, gpsimd = nc.sync, nc.scalar, nc.gpsimd
     with ExitStack() as ctx:
         held = ctx.enter_context(tc.tile_pool(name="held", bufs=1))
-        per_expert = ctx.enter_context(tc.tile_pool(name="per_expert", bufs=E))
-        picked = ctx.enter_context(tc.tile_pool(name="picked", bufs=2))
-        psum_a = ctx.enter_context(tc.psum_pool(name="psum_a", bufs=3))
-        psum_t = ctx.enter_context(tc.psum_pool(name="psum_t", bufs=3))
-        psum_y = ctx.enter_context(tc.psum_pool(name="psum_y", bufs=2))
+        psum = ctx.enter_context(tc.psum_pool(name="psum", bufs=1))
 
         offs_sb = held.tile([P, SLOTS // STRIPE], U16, name="offs_sb")
         dst_sb = held.tile([P, SLOTS // STRIPE], U16, name="dst_sb")
         tok_words = held.tile([P, T], I32, name="tok_words", align_bytes=64)
         tok_scales = held.tile([P, T], U8, name="tok_scales", align_bytes=64)
-        w1w = [held.tile([P, 2 * H], U8, name="w1w%d" % e, align_bytes=64) for e in range(E)]
+        w1w = {grp.start: held.tile([P, len(grp), 2 * H], U8, name="w1w%d" % grp.start, align_bytes=64) for grp in W1_LOADS}
+        w1w_of = {e: w1w[grp.start][:, e - grp.start, :] for grp in W1_LOADS for e in grp}
         w1s = [held.tile([P, len(grp), H], U8, name="w1s%d" % g, align_bytes=64) for g, grp in enumerate(W1_PLANES)]
         w1s_of = {e: w1s[g][:, e - grp.start, :] for g, grp in enumerate(W1_PLANES) for e in grp}
         w2w = held.tile([P, E * PASSES, 2 * N], U8, name="w2w", align_bytes=64)
@@ -76,166 +69,252 @@ def tile_moe_two_mlp_silu_kernel(
             for group in W1_PLANES
         ]
 
-        def load_w1_words(queue, e):
-            queue.dma_start(out=w1w[e][:].bitcast(I32), in_=w1_words.bitcast(I32)[e, 0])
+        def load_w1_words(queue, lo, hi):
+            src = w1_words.bitcast(I32)[lo:hi, 0].rearrange("e p b -> p e b")
+            queue.dma_start(out=w1w[lo][:].bitcast(I32), in_=src)
 
-        def load_w2_words(lo, hi):
+        def load_w2_words(queue, lo, hi):
             src = w2_words.bitcast(I32)[lo:hi].rearrange("e s p b -> p (e s) b")
-            sync.dma_start(out=w2w[:, lo * PASSES:hi * PASSES, :].bitcast(I32), in_=src)
+            queue.dma_start(out=w2w[:, lo * PASSES:hi * PASSES, :].bitcast(I32), in_=src)
 
-        def load_gate(lo, hi):
-            sync.dma_start(out=gate_sb[:, lo:hi], in_=gate[:, lo:hi])
+        def load_gate(queue, lo, hi):
+            queue.dma_start(out=gate_sb[:, lo:hi], in_=gate[:, lo:hi])
 
         nc.vector.memset(tok_scales[:].bitcast(I32), 0)
         nc.vector.memset(zero[:], 0.0)
-        for plane in (w1s[0], w2s, w1s[1]):
-            nc.vector.memset(plane[:].bitcast(I32), 0)
+        nc.vector.memset(w1s[0][:].bitcast(I32), 0)
+        nc.vector.memset(w2s[:].bitcast(I32), 0)
+        nc.vector.memset(w1s[1][:].bitcast(I32), 0)
         make_identity(nc, ident[:])
 
         sync.dma_start(offs_sb[:], offs)
-        sync.dma_start(dst_sb[:], dst)
-        load_w1_words(scalar, 0)
+        load_gate(sync, 0 * C, 1 * C)
+        load_w1_words(scalar, 0, 1)
         load_rows(scalar, tok_scales, x_rows, (0, 1,))
         load_rows(sync, tok_scales, x_rows, (2, 3,))
         sync.dma_start(out=tok_words[:], in_=x_words[0].rearrange("p t r -> p (t r)").bitcast(I32))
         load_rows(sync, w1s[0], w1_rows[0], (0, 1,))
-        nc.scalar.activation(out=out_sb[:], in_=zero[:, 0:1].to_broadcast([P, T]), func=SILU)
+        nc.scalar.activation(out=out_sb[:, 0:1536], in_=zero[:, 0:1].to_broadcast([P, 1536]), func=SILU)
         load_rows(scalar, w1s[0], w1_rows[0], (2, 3,))
         load_rows(gpsimd, w2s, w2_rows, (0,))
-        load_w1_words(sync, 1)
-        load_w1_words(sync, 2)
+        load_w1_words(sync, 1, 2)
+        load_w1_words(sync, 2, 3)
         load_rows(scalar, w2s, w2_rows, (1,))
         load_rows(sync, w1s[1], w1_rows[1], (0, 1,))
         load_rows(scalar, w1s[1], w1_rows[1], (2, 3,))
         load_rows(scalar, w2s, w2_rows, (2,))
         load_rows(sync, w2s, w2_rows, (3,))
-        load_w1_words(sync, 3)
-        load_w1_words(sync, 4)
-        load_w1_words(sync, 5)
-        load_w2_words(0, 4)
-        load_gate(0 * C, 2 * C)
-        load_w1_words(sync, 6)
-        load_w1_words(sync, 7)
-        load_gate(2 * C, 8 * C)
-        load_w2_words(4, 8)
+        load_w1_words(sync, 3, 4)
+        load_w1_words(sync, 4, 5)
+        load_w1_words(sync, 5, 6)
+        load_w2_words(sync, 0, 4)
+        load_gate(sync, 1 * C, 2 * C)
+        sync.dma_start(dst_sb[:], dst)
+        load_w1_words(sync, 6, 7)
+        load_w1_words(sync, 7, 8)
+        load_gate(sync, 2 * C, 8 * C)
+        load_w2_words(sync, 4, 8)
+
+        warm_in = held.tile([P, 4 * WARM_COLUMNS // C, C], BF16, name="warm_in", align_bytes=64)
+        warm_codes = held.tile([P, WARM_COLUMNS], U32, name="warm_codes", align_bytes=64)
+        warm_scales = held.tile([P, WARM_COLUMNS], U8, name="warm_scales", align_bytes=64)
+        nc.vector.tensor_copy(warm_in[:], gate_sb[:, 0:C].unsqueeze(1).to_broadcast([P, 4 * WARM_COLUMNS // C, C]))
+        nc.vector.quantize_mx(
+            out=warm_codes[:].bitcast(FP8X4), scales=warm_scales[:], in_=warm_in[:].rearrange("p a c -> p (a c)")
+        )
+        unread = psum.tile([P, WARM_COLUMNS], F32, name="unread", offset=7 * BANK)
+        for turn_number in range(WARM_PASSES):
+            nc.tensor.matmul_mx(
+                out=unread[:],
+                lhsT=warm_codes[:, 0:C].bitcast(FP8X4),
+                lhsT_scale=warm_scales[:, 0:C],
+                rhs=w1w_of[0][:, 0:2 * WARM_COLUMNS].bitcast(FP4X4),
+                rhs_scale=warm_scales[:],
+                start=True,
+                stop=True,
+            )
 
         slot_words = held.tile([P, SLOTS], U32, name="slot_words", align_bytes=64)
-        scales_of = {}
-        h_of = {}
-        grouped_of = {}
-        codes_of = {}
+        slot_scales = held.tile([P, SLOTS - C], U8, name="slot_scales", align_bytes=64)
+        h = [held.tile([P, H], BF16, name="h%d" % e, align_bytes=64) for e in range(E)]
+        grouped, codes, scales = {}, {}, {}
+        for grp in QUANTISED:
+            g = held.tile([P, len(grp) * H], BF16, name="grouped%d" % grp.start, align_bytes=64)
+            c = held.tile([P, len(grp) * PASSES * C], U32, name="codes%d" % grp.start, align_bytes=64)
+            z = held.tile([P, len(grp) * PASSES * C], U8, name="scales%d" % grp.start, align_bytes=64)
+            for e in grp:
+                grouped[e], codes[e], scales[e] = g, c, z
+        first_of = {e: grp.start for grp in QUANTISED for e in grp}
+        sums = {}
+        turned = {}
+        ys = {}
 
-        def picks(experts):
-            return offs_sb[:, experts.start * C // STRIPE:experts.stop * C // STRIPE]
+        def scale_place(slot):
+            return slot - FIRST_SCALES if slot >= FIRST_SCALES else slot + SLOTS - FIRST_SCALES - C
 
-        def gather_scales(experts):
-            slot_scales = picked.tile([P, len(experts) * C], U8, name="slot_scales", align_bytes=64)
-            nc.vector.tensor_copy(slot_scales[:], tok_scales[:].indirect(picks(experts)))
+        def gather_scales(lo, hi):
+            at = scale_place(lo)
+            nc.vector.tensor_copy(slot_scales[:, at:at + hi - lo], tok_scales[:].indirect(offs_sb[:, lo // STRIPE:hi // STRIPE]))
+
+        def gather_words(lo, hi):
+            picks = offs_sb[:, lo // STRIPE:hi // STRIPE]
+            nc.vector.tensor_copy(slot_words[:, lo:hi], tok_words[:].bitcast(U32).indirect(picks))
+
+        def first_matmul(e, s, bank):
+            a = psum.tile([P, PASS], F32, name="a%d_%d" % (e, s), offset=bank * BANK)
+            nc.tensor.matmul_mx(
+                out=a[:],
+                lhsT=slot_words[:, e * C:(e + 1) * C].bitcast(FP8X4),
+                lhsT_scale=slot_scales[:, scale_place(e * C):scale_place(e * C) + C],
+                rhs=w1w_of[e][:, 2 * s * PASS:2 * (s + 1) * PASS].bitcast(FP4X4),
+                rhs_scale=w1s_of[e][:, s * PASS:(s + 1) * PASS],
+                start=True,
+                stop=True,
+            )
+            sums[e, s] = a
+
+        def silu(e, s):
+            nc.scalar.activation(
+                out=h[e][:, s * PASS:(s + 1) * PASS].rearrange("c (u m d) -> c u m d", u=2, d=2),
+                in_=sums[e, s][:].rearrange("c (m u d) -> c u m d", u=2, d=2),
+                func=SILU,
+            )
+
+        def turn(e, piece, bank):
+            pairs = h[e][:].bitcast(F32)
+            tile = psum.tile([P, len(piece), 2, C], F32, name="turned%d_%d" % (e, piece.start), offset=bank * BANK)
+            for s in piece:
+                for u in range(2):
+                    first = (2 * s + u) * P
+                    nc.tensor.transpose(tile[:, s - piece.start, u, :], pairs[:, first:first + P], ident[:])
+            turned[e, piece.start] = tile
+
+        def regroup(engine, e, piece):
+            at = (e - first_of[e]) * PASSES
+            words = grouped[e][:].bitcast(F32)[:, (at + piece.start) * 2 * C:(at + piece.stop) * 2 * C]
+            side_by_side = words.rearrange("p (s c u) -> p s c u", s=len(piece), u=2)
+            apart = turned[e, piece.start][:].rearrange("p s u c -> p s c u")
+            if engine is nc.scalar:
+                nc.scalar.copy(out=side_by_side, in_=apart)
+            else:
+                nc.vector.tensor_copy(out=side_by_side, in_=apart)
+
+        def quantise(e, piece):
+            at = (e - first_of[e]) * PASSES
+            lo, hi = (at + piece.start) * C, (at + piece.stop) * C
+            nc.vector.quantize_mx(
+                out=codes[e][:, lo:hi].bitcast(FP8X4), scales=scales[e][:, lo:hi], in_=grouped[e][:, 4 * lo:4 * hi]
+            )
+
+        def second_layer(experts, bank):
+            y = psum.tile([P, len(experts) * C], F32, name="y%d" % experts.start, offset=bank * BANK)
             for e in experts:
-                scales_of[e] = slot_scales[:, (e - experts.start) * C:(e - experts.start + 1) * C]
-
-        def gather_words(experts):
-            cols = slice(experts.start * C, experts.stop * C)
-            nc.vector.tensor_copy(slot_words[:, cols], tok_words[:].bitcast(U32).indirect(picks(experts)))
-
-        def first_layer(e):
-            h = per_expert.tile([P, H], BF16, name="h", align_bytes=64)
-            for s in range(PASSES):
-                a = psum_a.tile([P, PASS], F32, name="a")
-                nc.tensor.matmul_mx(
-                    out=a[:],
-                    lhsT=slot_words[:, e * C:(e + 1) * C].bitcast(FP8X4),
-                    lhsT_scale=scales_of[e],
-                    rhs=w1w[e][:, 2 * s * PASS:2 * (s + 1) * PASS].bitcast(FP4X4),
-                    rhs_scale=w1s_of[e][:, s * PASS:(s + 1) * PASS],
-                    start=True,
-                    stop=True,
-                )
-                nc.scalar.activation(
-                    out=h[:, s * PASS:(s + 1) * PASS].rearrange("c (u m d) -> c u m d", u=2, d=2),
-                    in_=a[:].rearrange("c (m u d) -> c u m d", u=2, d=2),
-                    func=SILU,
-                )
-            h_of[e] = h
-
-        def pieces(e):
-            return [range(s, s + 1) for s in range(PASSES)] if e == E - 1 else [range(PASSES)]
-
-        def turn(e):
-            pairs = h_of[e][:].bitcast(F32)
-            grouped = per_expert.tile([P, PASSES * C * 4], BF16, name="grouped", align_bytes=64)
-            for piece in pieces(e):
-                turned = psum_t.tile([P, len(piece), 2, C], F32, name="turned")
-                for s in piece:
-                    for u in range(2):
-                        first = (2 * s + u) * P
-                        nc.tensor.transpose(turned[:, s - piece.start, u, :], pairs[:, first:first + P], ident[:])
-                words = grouped[:].bitcast(F32)[:, piece.start * 2 * C:piece.stop * 2 * C]
-                side_by_side = words.rearrange("p (s c u) -> p s c u", s=len(piece), u=2)
-                apart = turned[:].rearrange("p s u c -> p s c u")
-                if e in TURNED_ON_SCALAR:
-                    nc.scalar.copy(out=side_by_side, in_=apart)
-                else:
-                    nc.vector.tensor_copy(out=side_by_side, in_=apart)
-            grouped_of[e] = grouped
-
-        def quantise(e):
-            codes = per_expert.tile([P, PASSES * C], U32, name="codes", align_bytes=64)
-            scales = per_expert.tile([P, PASSES * C], U8, name="scales", align_bytes=64)
-            for piece in pieces(e):
-                lo, hi = piece.start * C, piece.stop * C
-                nc.vector.quantize_mx(
-                    out=codes[:, lo:hi].bitcast(FP8X4), scales=scales[:, lo:hi], in_=grouped_of[e][:, 4 * lo:4 * hi]
-                )
-            codes_of[e] = (codes, scales)
-
-        def second_layer(experts):
-            y = psum_y.tile([P, len(experts) * C], F32, name="y")
-            for e in experts:
-                codes, scales = codes_of[e]
                 place = (e - experts.start) * C
                 for s in range(PASSES):
+                    at = ((e - first_of[e]) * PASSES + s) * C
                     nc.tensor.matmul_mx(
                         out=y[:, place:place + C],
                         lhsT=w2w[:, e * PASSES + s, :].bitcast(FP4X4),
                         lhsT_scale=w2s[:, e * PASSES + s, :],
-                        rhs=codes[:, s * C:(s + 1) * C].bitcast(FP8X4),
-                        rhs_scale=scales[:, s * C:(s + 1) * C],
+                        rhs=codes[e][:, at:at + C].bitcast(FP8X4),
+                        rhs_scale=scales[e][:, at:at + C],
                         start=(s == 0),
                         stop=(s == PASSES - 1),
                     )
-            cols = slice(experts.start * C, experts.stop * C)
-            if experts.start < FIRST_Y_ON_SCALAR:
-                nc.vector.tensor_tensor(y_sb[:, cols], y[:], gate_sb[:, cols], MULT)
-            else:
-                nc.scalar.copy(out=y_sb[:, cols], in_=y[:])
+            ys[experts.start] = y
 
-        def scatter(lo):
-            hi = lo + SCATTER
+        def take_y(with_gate, experts):
+            cols = slice(experts.start * C, experts.stop * C)
+            if with_gate:
+                nc.vector.tensor_tensor(y_sb[:, cols], ys[experts.start][:], gate_sb[:, cols], MULT)
+            else:
+                nc.scalar.copy(out=y_sb[:, cols], in_=ys[experts.start][:])
+
+        def scatter(lo, hi, gated):
             places = dst_sb[:, lo // STRIPE:hi // STRIPE]
-            if lo < FIRST_Y_ON_SCALAR * C:
+            if gated:
                 nc.vector.tensor_copy(out_sb[:].indirect(places), y_sb[:, lo:hi])
             else:
                 nc.vector.tensor_tensor(out_sb[:].indirect(places), y_sb[:, lo:hi], gate_sb[:, lo:hi], MULT)
 
-        for step in range(E + LAG_SECOND + LAG_SCATTER):
-            for experts, at in SCALE_GATHERS:
-                if at == step:
-                    gather_scales(experts)
-            if step == 0:
-                for experts in WORD_GATHERS:
-                    gather_words(experts)
-            if step < E:
-                first_layer(step)
-            if 0 <= step - LAG_TURN < E:
-                turn(step - LAG_TURN)
-            if 0 <= step - LAG_QUANTISE < E:
-                quantise(step - LAG_QUANTISE)
-            for experts in Y_GROUPS:
-                if experts[-1] + LAG_SECOND == step:
-                    second_layer(experts)
-            for lo in range(0, SLOTS, SCATTER):
-                if (lo + SCATTER) // C - 1 + LAG_SECOND + LAG_SCATTER == step:
-                    scatter(lo)
+        gather_scales(0, 384)
+        gather_words(0, 256)
+        gather_words(256, 1024)
+        first_matmul(0, 0, 0)
+        silu(0, 0)
+        first_matmul(0, 1, 1)
+        silu(0, 1)
+        first_matmul(1, 0, 2)
+        silu(1, 0)
+        first_matmul(1, 1, 0)
+        silu(1, 1)
+        turn(0, range(0, 2), 3)
+        regroup(nc.scalar, 0, range(0, 2))
+        gather_scales(384, 1024)
+        first_matmul(2, 0, 1)
+        silu(2, 0)
+        first_matmul(2, 1, 2)
+        silu(2, 1)
+        turn(1, range(0, 2), 4)
+        regroup(nc.vector, 1, range(0, 2))
+        quantise(0, range(0, 2))
+        first_matmul(3, 0, 0)
+        silu(3, 0)
+        first_matmul(3, 1, 1)
+        silu(3, 1)
+        turn(2, range(0, 2), 5)
+        regroup(nc.vector, 2, range(0, 2))
+        quantise(1, range(0, 2))
+        first_matmul(4, 0, 2)
+        silu(4, 0)
+        first_matmul(4, 1, 0)
+        silu(4, 1)
+        turn(3, range(0, 2), 3)
+        regroup(nc.vector, 3, range(0, 2))
+        quantise(2, range(0, 2))
+        second_layer(range(0, 2), 6)
+        take_y(True, range(0, 2))
+        first_matmul(5, 0, 1)
+        silu(5, 0)
+        first_matmul(5, 1, 2)
+        silu(5, 1)
+        turn(4, range(0, 2), 4)
+        regroup(nc.scalar, 4, range(0, 2))
+        quantise(3, range(0, 2))
+        scatter(0, 256, True)
+        first_matmul(6, 0, 0)
+        silu(6, 0)
+        first_matmul(6, 1, 1)
+        silu(6, 1)
+        turn(5, range(0, 2), 5)
+        regroup(nc.vector, 5, range(0, 2))
+        quantise(4, range(0, 2))
+        second_layer(range(2, 4), 7)
+        take_y(True, range(2, 4))
+        first_matmul(7, 0, 2)
+        silu(7, 0)
+        first_matmul(7, 1, 0)
+        silu(7, 1)
+        turn(6, range(0, 2), 3)
+        regroup(nc.scalar, 6, range(0, 2))
+        quantise(5, range(0, 2))
+        second_layer(range(4, 5), 6)
+        take_y(False, range(4, 5))
+        scatter(256, 512, True)
+        turn(7, range(0, 1), 4)
+        regroup(nc.scalar, 7, range(0, 1))
+        turn(7, range(1, 2), 5)
+        regroup(nc.scalar, 7, range(1, 2))
+        quantise(6, range(0, 2))
+        second_layer(range(5, 6), 7)
+        take_y(False, range(5, 6))
+        quantise(7, range(0, 1))
+        quantise(7, range(1, 2))
+        second_layer(range(6, 7), 6)
+        take_y(False, range(6, 7))
+        scatter(512, 768, False)
+        second_layer(range(7, 8), 7)
+        take_y(False, range(7, 8))
+        scatter(768, 1024, False)
 
         sync.dma_start(out=out, in_=out_sb[:])

@@ -29,6 +29,7 @@ W1_PLANES = (range(0, 3), range(3, 8),)
 W1_LOADS = (range(0, 1), range(1, 2), range(2, 3), range(3, 4), range(4, 5), range(5, 6), range(6, 7), range(7, 8),)
 QUANTISED = (range(0, 1), range(1, 2), range(2, 3), range(3, 4), range(4, 5), range(5, 6), range(6, 7), range(7, 8),)
 FIRST_SCALES = 384
+WARM_GATES = 32
 BANK = 2048
 WARM_PASSES, WARM_COLUMNS = 5, 256
 
@@ -88,7 +89,7 @@ def tile_moe_two_mlp_silu_kernel(
         make_identity(nc, ident[:])
 
         sync.dma_start(offs_sb[:], offs)
-        load_gate(sync, 0 * C, 1 * C)
+        load_gate(sync, 0, WARM_GATES)
         load_w1_words(scalar, 0, 1)
         load_rows(scalar, tok_scales, x_rows, (0, 1,))
         load_rows(sync, tok_scales, x_rows, (2, 3,))
@@ -108,17 +109,17 @@ def tile_moe_two_mlp_silu_kernel(
         load_w1_words(sync, 4, 5)
         load_w1_words(sync, 5, 6)
         load_w2_words(sync, 0, 4)
-        load_gate(sync, 1 * C, 2 * C)
+        load_gate(sync, WARM_GATES, 2 * C)
         sync.dma_start(dst_sb[:], dst)
         load_w1_words(sync, 6, 7)
         load_w1_words(sync, 7, 8)
         load_gate(sync, 2 * C, 8 * C)
         load_w2_words(sync, 4, 8)
 
-        warm_in = held.tile([P, 4 * WARM_COLUMNS // C, C], BF16, name="warm_in", align_bytes=64)
+        warm_in = held.tile([P, 4 * WARM_COLUMNS // WARM_GATES, WARM_GATES], BF16, name="warm_in", align_bytes=64)
         warm_codes = held.tile([P, WARM_COLUMNS], U32, name="warm_codes", align_bytes=64)
         warm_scales = held.tile([P, WARM_COLUMNS], U8, name="warm_scales", align_bytes=64)
-        nc.vector.tensor_copy(warm_in[:], gate_sb[:, 0:C].unsqueeze(1).to_broadcast([P, 4 * WARM_COLUMNS // C, C]))
+        nc.vector.tensor_copy(warm_in[:], gate_sb[:, 0:WARM_GATES].unsqueeze(1).to_broadcast([P, 4 * WARM_COLUMNS // WARM_GATES, WARM_GATES]))
         nc.vector.quantize_mx(
             out=warm_codes[:].bitcast(FP8X4), scales=warm_scales[:], in_=warm_in[:].rearrange("p a c -> p (a c)")
         )
@@ -298,7 +299,7 @@ def tile_moe_two_mlp_silu_kernel(
         turn(6, range(0, 2), 3)
         regroup(nc.scalar, 6, range(0, 2))
         quantise(5, range(0, 2))
-        second_layer(range(4, 5), 6)
+        second_layer(range(4, 5), 1)
         take_y(False, range(4, 5))
         scatter(256, 512, True)
         turn(7, range(0, 1), 4)
@@ -306,7 +307,7 @@ def tile_moe_two_mlp_silu_kernel(
         turn(7, range(1, 2), 5)
         regroup(nc.scalar, 7, range(1, 2))
         quantise(6, range(0, 2))
-        second_layer(range(5, 6), 7)
+        second_layer(range(5, 6), 2)
         take_y(False, range(5, 6))
         quantise(7, range(0, 1))
         quantise(7, range(1, 2))

@@ -16,7 +16,9 @@ U8 = mybir.dt.uint8
 FP8X4 = mybir.dt.float8_e4m3fn_x4
 FP4X4 = mybir.dt.float4_e2m1fn_x4
 SILU = mybir.ActivationFunctionType.Silu
+COPY = mybir.ActivationFunctionType.Copy
 MULT = mybir.AluOpType.mult
+ADD = mybir.AluOpType.add
 
 P = 128
 PASS = 512
@@ -27,7 +29,6 @@ ROWS = 4
 
 W1_PLANES = (range(0, 3), range(3, 8),)
 W1_LOADS = (range(0, 1), range(1, 2), range(2, 3), range(3, 4), range(4, 5), range(5, 6), range(6, 7), range(7, 8),)
-QUANTISED = (range(0, 1), range(1, 2), range(2, 3), range(3, 4), range(4, 5), range(5, 6), range(6, 7), range(7, 8),)
 FIRST_SCALES = 384
 WARM_GATES = 32
 BANK = 2048
@@ -136,37 +137,38 @@ def tile_moe_two_mlp_silu_kernel(
             )
 
         slot_words = held.tile([P, SLOTS], U32, name="slot_words", align_bytes=64)
-        slot_scales = held.tile([P, SLOTS - C], U8, name="slot_scales", align_bytes=64)
-        h = [held.tile([P, H], BF16, name="h%d" % e, align_bytes=64) for e in range(E)]
-        grouped, codes, scales = {}, {}, {}
-        for grp in QUANTISED:
-            g = held.tile([P, len(grp) * H], BF16, name="grouped%d" % grp.start, align_bytes=64)
-            c = held.tile([P, len(grp) * PASSES * C], U32, name="codes%d" % grp.start, align_bytes=64)
-            z = held.tile([P, len(grp) * PASSES * C], U8, name="scales%d" % grp.start, align_bytes=64)
-            for e in grp:
-                grouped[e], codes[e], scales[e] = g, c, z
-        first_of = {e: grp.start for grp in QUANTISED for e in grp}
+        slot_scales = held.tile([P, SLOTS], U8, name="slot_scales", align_bytes=64)
+        arena = ctx.enter_context(tc.tile_pool(name="arena", bufs=1))
+        h = {}
+        grouped = [held.tile([P, H], BF16, name="grouped%d" % e, align_bytes=64) for e in range(E)]
+        scales = [held.tile([P, PASSES * C], U8, name="scales%d" % e, align_bytes=64) for e in range(E)]
+        codes = {}
         sums = {}
         turned = {}
         ys = {}
+        HELD = {}
 
-        def scale_place(slot):
-            return slot - FIRST_SCALES if slot >= FIRST_SCALES else slot + SLOTS - FIRST_SCALES - C
+        WORDS = ((0, 256, 0), (256, 1024, 256))
+        SCALES = ((0, 384, 512), (384, 1024, 0))
 
-        def gather_scales(lo, hi):
-            at = scale_place(lo)
+        def place(pieces, slot):
+            return [at + slot - lo for lo, hi, at in pieces if lo <= slot < hi][0]
+
+        def gather_scales(n):
+            lo, hi, at = SCALES[n]
             nc.vector.tensor_copy(slot_scales[:, at:at + hi - lo], tok_scales[:].indirect(offs_sb[:, lo // STRIPE:hi // STRIPE]))
 
-        def gather_words(lo, hi):
+        def gather_words(n):
+            lo, hi, at = WORDS[n]
             picks = offs_sb[:, lo // STRIPE:hi // STRIPE]
-            nc.vector.tensor_copy(slot_words[:, lo:hi], tok_words[:].bitcast(U32).indirect(picks))
+            nc.vector.tensor_copy(slot_words[:, at:at + hi - lo], tok_words[:].bitcast(U32).indirect(picks))
 
         def first_matmul(e, s, bank):
             a = psum.tile([P, PASS], F32, name="a%d_%d" % (e, s), offset=bank * BANK)
             nc.tensor.matmul_mx(
                 out=a[:],
-                lhsT=slot_words[:, e * C:(e + 1) * C].bitcast(FP8X4),
-                lhsT_scale=slot_scales[:, scale_place(e * C):scale_place(e * C) + C],
+                lhsT=slot_words[:, place(WORDS, e * C):place(WORDS, e * C) + C].bitcast(FP8X4),
+                lhsT_scale=slot_scales[:, place(SCALES, e * C):place(SCALES, e * C) + C],
                 rhs=w1w_of[e][:, 2 * s * PASS:2 * (s + 1) * PASS].bitcast(FP4X4),
                 rhs_scale=w1s_of[e][:, s * PASS:(s + 1) * PASS],
                 start=True,
@@ -175,24 +177,27 @@ def tile_moe_two_mlp_silu_kernel(
             sums[e, s] = a
 
         def silu(e, s):
+            h[e, s] = arena.tile([P, PASS], BF16, name="h%d_%d" % (e, s), align_bytes=64, offset=(e * PASSES + s) * 2 * PASS)
             nc.scalar.activation(
-                out=h[e][:, s * PASS:(s + 1) * PASS].rearrange("c (u m d) -> c u m d", u=2, d=2),
+                out=h[e, s][:].rearrange("c (u m d) -> c u m d", u=2, d=2),
                 in_=sums[e, s][:].rearrange("c (m u d) -> c u m d", u=2, d=2),
                 func=SILU,
             )
 
+        def first(e, s, bank):
+            first_matmul(e, s, bank)
+            silu(e, s)
+
         def turn(e, piece, bank):
-            pairs = h[e][:].bitcast(F32)
             tile = psum.tile([P, len(piece), 2, C], F32, name="turned%d_%d" % (e, piece.start), offset=bank * BANK)
             for s in piece:
+                pairs = h[e, s][:].bitcast(F32)
                 for u in range(2):
-                    first = (2 * s + u) * P
-                    nc.tensor.transpose(tile[:, s - piece.start, u, :], pairs[:, first:first + P], ident[:])
+                    nc.tensor.transpose(tile[:, s - piece.start, u, :], pairs[:, u * P:(u + 1) * P], ident[:])
             turned[e, piece.start] = tile
 
         def regroup(engine, e, piece):
-            at = (e - first_of[e]) * PASSES
-            words = grouped[e][:].bitcast(F32)[:, (at + piece.start) * 2 * C:(at + piece.stop) * 2 * C]
+            words = grouped[e][:].bitcast(F32)[:, piece.start * 2 * C:piece.stop * 2 * C]
             side_by_side = words.rearrange("p (s c u) -> p s c u", s=len(piece), u=2)
             apart = turned[e, piece.start][:].rearrange("p s u c -> p s c u")
             if engine is nc.scalar:
@@ -201,8 +206,12 @@ def tile_moe_two_mlp_silu_kernel(
                 nc.vector.tensor_copy(out=side_by_side, in_=apart)
 
         def quantise(e, piece):
-            at = (e - first_of[e]) * PASSES
-            lo, hi = (at + piece.start) * C, (at + piece.stop) * C
+            if e not in codes:
+                if e in HELD:
+                    codes[e] = arena.tile([P, PASSES * C], U32, name="codes%d" % e, align_bytes=64, offset=HELD[e] * 2 * PASS)
+                else:
+                    codes[e] = held.tile([P, PASSES * C], U32, name="codes%d" % e, align_bytes=64)
+            lo, hi = piece.start * C, piece.stop * C
             nc.vector.quantize_mx(
                 out=codes[e][:, lo:hi].bitcast(FP8X4), scales=scales[e][:, lo:hi], in_=grouped[e][:, 4 * lo:4 * hi]
             )
@@ -212,110 +221,97 @@ def tile_moe_two_mlp_silu_kernel(
             for e in experts:
                 place = (e - experts.start) * C
                 for s in range(PASSES):
-                    at = ((e - first_of[e]) * PASSES + s) * C
                     nc.tensor.matmul_mx(
                         out=y[:, place:place + C],
                         lhsT=w2w[:, e * PASSES + s, :].bitcast(FP4X4),
                         lhsT_scale=w2s[:, e * PASSES + s, :],
-                        rhs=codes[e][:, at:at + C].bitcast(FP8X4),
-                        rhs_scale=scales[e][:, at:at + C],
+                        rhs=codes[e][:, s * C:(s + 1) * C].bitcast(FP8X4),
+                        rhs_scale=scales[e][:, s * C:(s + 1) * C],
                         start=(s == 0),
                         stop=(s == PASSES - 1),
                     )
             ys[experts.start] = y
 
-        def take_y(with_gate, experts):
+        def take_y(experts, with_gate=True):
             cols = slice(experts.start * C, experts.stop * C)
             if with_gate:
                 nc.vector.tensor_tensor(y_sb[:, cols], ys[experts.start][:], gate_sb[:, cols], MULT)
             else:
                 nc.scalar.copy(out=y_sb[:, cols], in_=ys[experts.start][:])
 
-        def scatter(lo, hi, gated):
-            places = dst_sb[:, lo // STRIPE:hi // STRIPE]
-            if gated:
-                nc.vector.tensor_copy(out_sb[:].indirect(places), y_sb[:, lo:hi])
+        def scatter(how, lo, hi):
+            places = out_sb[:].indirect(dst_sb[:, lo // STRIPE:hi // STRIPE])
+            if how == "scalar":
+                nc.scalar.activation(places, y_sb[:, lo:hi], COPY)
+            elif how == "copy":
+                nc.vector.tensor_copy(places, y_sb[:, lo:hi])
             else:
-                nc.vector.tensor_tensor(out_sb[:].indirect(places), y_sb[:, lo:hi], gate_sb[:, lo:hi], MULT)
+                nc.vector.tensor_tensor(places, y_sb[:, lo:hi], gate_sb[:, lo:hi], MULT)
 
-        gather_scales(0, 384)
-        gather_words(0, 256)
-        gather_words(256, 1024)
-        first_matmul(0, 0, 0)
-        silu(0, 0)
-        first_matmul(0, 1, 1)
-        silu(0, 1)
-        first_matmul(1, 0, 2)
-        silu(1, 0)
-        first_matmul(1, 1, 0)
-        silu(1, 1)
-        turn(0, range(0, 2), 3)
-        regroup(nc.scalar, 0, range(0, 2))
-        gather_scales(384, 1024)
-        first_matmul(2, 0, 1)
-        silu(2, 0)
-        first_matmul(2, 1, 2)
-        silu(2, 1)
-        turn(1, range(0, 2), 4)
-        regroup(nc.vector, 1, range(0, 2))
-        quantise(0, range(0, 2))
-        first_matmul(3, 0, 0)
-        silu(3, 0)
-        first_matmul(3, 1, 1)
-        silu(3, 1)
-        turn(2, range(0, 2), 5)
-        regroup(nc.vector, 2, range(0, 2))
-        quantise(1, range(0, 2))
-        first_matmul(4, 0, 2)
-        silu(4, 0)
-        first_matmul(4, 1, 0)
-        silu(4, 1)
-        turn(3, range(0, 2), 3)
-        regroup(nc.vector, 3, range(0, 2))
-        quantise(2, range(0, 2))
+        both, one, two = range(0, 2), range(0, 1), range(1, 2)
+        V, S = nc.vector, nc.scalar
+        gather_scales(0)
+        gather_words(0)
+        gather_words(1)
+        first(0, 0, 0)
+        first(0, 1, 1)
+        first(1, 0, 2)
+        first(1, 1, 0)
+        turn(0, both, 3)
+        regroup(S, 0, both)
+        gather_scales(1)
+        first(2, 0, 1)
+        first(2, 1, 2)
+        turn(1, both, 4)
+        regroup(V, 1, both)
+        quantise(0, both)
+        first(3, 0, 0)
+        first(3, 1, 1)
+        turn(2, both, 5)
+        regroup(V, 2, both)
+        quantise(1, both)
+        first(4, 0, 2)
+        first(4, 1, 0)
+        turn(3, both, 3)
+        regroup(V, 3, both)
+        quantise(2, both)
         second_layer(range(0, 2), 6)
-        take_y(True, range(0, 2))
-        first_matmul(5, 0, 1)
-        silu(5, 0)
-        first_matmul(5, 1, 2)
-        silu(5, 1)
-        turn(4, range(0, 2), 4)
-        regroup(nc.scalar, 4, range(0, 2))
-        quantise(3, range(0, 2))
-        scatter(0, 256, True)
-        first_matmul(6, 0, 0)
-        silu(6, 0)
-        first_matmul(6, 1, 1)
-        silu(6, 1)
-        turn(5, range(0, 2), 5)
-        regroup(nc.vector, 5, range(0, 2))
-        quantise(4, range(0, 2))
+        take_y(range(0, 2))
+        first(5, 0, 1)
+        first(5, 1, 2)
+        turn(4, both, 4)
+        regroup(S, 4, both)
+        quantise(3, both)
+        scatter("copy", 0, 256)
+        first(6, 0, 0)
+        first(6, 1, 1)
+        turn(5, both, 5)
+        regroup(V, 5, both)
+        quantise(4, both)
         second_layer(range(2, 4), 7)
-        take_y(True, range(2, 4))
-        first_matmul(7, 0, 2)
-        silu(7, 0)
-        first_matmul(7, 1, 0)
-        silu(7, 1)
-        turn(6, range(0, 2), 3)
-        regroup(nc.scalar, 6, range(0, 2))
-        quantise(5, range(0, 2))
+        take_y(range(2, 4))
+        first(7, 0, 2)
+        first(7, 1, 0)
+        turn(6, both, 3)
+        regroup(S, 6, both)
+        quantise(5, both)
+        scatter("copy", 256, 512)
         second_layer(range(4, 5), 1)
-        take_y(False, range(4, 5))
-        scatter(256, 512, True)
-        turn(7, range(0, 1), 4)
-        regroup(nc.scalar, 7, range(0, 1))
-        turn(7, range(1, 2), 5)
-        regroup(nc.scalar, 7, range(1, 2))
-        quantise(6, range(0, 2))
+        take_y(range(4, 5))
+        turn(7, one, 4)
+        regroup(S, 7, one)
+        turn(7, two, 5)
+        regroup(S, 7, two)
         second_layer(range(5, 6), 2)
-        take_y(False, range(5, 6))
-        quantise(7, range(0, 1))
-        quantise(7, range(1, 2))
+        take_y(range(5, 6))
+        scatter("scalar", 512, 768)
+        quantise(6, both)
+        quantise(7, one)
+        quantise(7, two)
         second_layer(range(6, 7), 6)
-        take_y(False, range(6, 7))
-        scatter(512, 768, False)
+        take_y(range(6, 7))
         second_layer(range(7, 8), 7)
-        take_y(False, range(7, 8))
-        scatter(768, 1024, False)
+        take_y(range(7, 8))
+        scatter("scalar", 768, 1024)
 
         sync.dma_start(out=out, in_=out_sb[:])

@@ -32,7 +32,7 @@ W1_LOADS = (range(0, 1), range(1, 2), range(2, 3), range(3, 4), range(4, 5), ran
 FIRST_SCALES = 384
 WARM_GATES = 32
 BANK = 2048
-WARM_PASSES, WARM_COLUMNS = 5, 256
+WARM_PASSES, WARM_COLUMNS = 4, 256
 
 
 def tile_moe_two_mlp_silu_kernel(
@@ -148,7 +148,7 @@ def tile_moe_two_mlp_silu_kernel(
         ys = {}
         HELD = {}
 
-        WORDS = ((0, 256, 0), (256, 1024, 256))
+        WORDS = ((0, 128, 0), (128, 384, 128), (384, 1024, 384))
         SCALES = ((0, 384, 512), (384, 1024, 0))
 
         def place(pieces, slot):
@@ -253,6 +253,7 @@ def tile_moe_two_mlp_silu_kernel(
         gather_scales(0)
         gather_words(0)
         gather_words(1)
+        gather_words(2)
         first(0, 0, 0)
         first(0, 1, 1)
         first(1, 0, 2)

@@ -32,7 +32,6 @@ W1_LOADS = (range(0, 1), range(1, 2), range(2, 3), range(3, 4), range(4, 5), ran
 FIRST_SCALES = 384
 WARM_GATES = 32
 BANK = 2048
-WARM_PASSES, WARM_COLUMNS = 4, 256
 
 
 def tile_moe_two_mlp_silu_kernel(
@@ -116,25 +115,6 @@ def tile_moe_two_mlp_silu_kernel(
         load_w1_words(sync, 7, 8)
         load_gate(sync, 2 * C, 8 * C)
         load_w2_words(sync, 4, 8)
-
-        warm_in = held.tile([P, 4 * WARM_COLUMNS // WARM_GATES, WARM_GATES], BF16, name="warm_in", align_bytes=64)
-        warm_codes = held.tile([P, WARM_COLUMNS], U32, name="warm_codes", align_bytes=64)
-        warm_scales = held.tile([P, WARM_COLUMNS], U8, name="warm_scales", align_bytes=64)
-        nc.vector.tensor_copy(warm_in[:], gate_sb[:, 0:WARM_GATES].unsqueeze(1).to_broadcast([P, 4 * WARM_COLUMNS // WARM_GATES, WARM_GATES]))
-        nc.vector.quantize_mx(
-            out=warm_codes[:].bitcast(FP8X4), scales=warm_scales[:], in_=warm_in[:].rearrange("p a c -> p (a c)")
-        )
-        unread = psum.tile([P, WARM_COLUMNS], F32, name="unread", offset=7 * BANK)
-        for turn_number in range(WARM_PASSES):
-            nc.tensor.matmul_mx(
-                out=unread[:],
-                lhsT=warm_codes[:, 0:C].bitcast(FP8X4),
-                lhsT_scale=warm_scales[:, 0:C],
-                rhs=w1w_of[0][:, 0:2 * WARM_COLUMNS].bitcast(FP4X4),
-                rhs_scale=warm_scales[:],
-                start=True,
-                stop=True,
-            )
 
         slot_words = held.tile([P, SLOTS], U32, name="slot_words", align_bytes=64)
         slot_scales = held.tile([P, SLOTS], U8, name="slot_scales", align_bytes=64)

from contextlib import ExitStack

import concourse.mybir as mybir
from concourse.masks import make_identity

K, T, E, C, H, N = 512, 1536, 8, 128, 1024, 128
SLOTS = E * C
FLOPS = 2 * SLOTS * (K * H + H * N)

F32 = mybir.dt.float32
BF16 = mybir.dt.bfloat16
I32 = mybir.dt.int32
U32 = mybir.dt.uint32
U16 = mybir.dt.uint16
U8 = mybir.dt.uint8
FP8X4 = mybir.dt.float8_e4m3fn_x4
FP4X4 = mybir.dt.float4_e2m1fn_x4
SILU = mybir.ActivationFunctionType.Silu
COPY = mybir.ActivationFunctionType.Copy
MULT = mybir.AluOpType.mult
ADD = mybir.AluOpType.add

P = 128
PASS = 512
PASSES = H // PASS
STRIPE = 16
QUADRANT = 32
ROWS = 4

W1_PLANES = (range(0, 3), range(3, 8),)
W1_LOADS = (range(0, 1), range(1, 2), range(2, 3), range(3, 4), range(4, 5), range(5, 6), range(6, 7), range(7, 8),)
FIRST_SCALES = 384
WARM_GATES = 32
BANK = 2048


def tile_moe_two_mlp_silu_kernel(
    tc, x_words, x_scales, w1_words, w1_scales, w2_words, w2_scales, gate, offs, dst, out
):
    nc = tc.nc
    sync, scalar, gpsimd = nc.sync, nc.scalar, nc.gpsimd
    with ExitStack() as ctx:
        held = ctx.enter_context(tc.tile_pool(name="held", bufs=1))
        psum = ctx.enter_context(tc.psum_pool(name="psum", bufs=1))

        offs_sb = held.tile([P, SLOTS // STRIPE], U16, name="offs_sb")
        dst_sb = held.tile([P, SLOTS // STRIPE], U16, name="dst_sb")
        tok_words = held.tile([P, T], I32, name="tok_words", align_bytes=64)
        tok_scales = held.tile([P, T], U8, name="tok_scales", align_bytes=64)
        w1w = {grp.start: held.tile([P, len(grp), 2 * H], U8, name="w1w%d" % grp.start, align_bytes=64) for grp in W1_LOADS}
        w1w_of = {e: w1w[grp.start][:, e - grp.start, :] for grp in W1_LOADS for e in grp}
        w1s = [held.tile([P, len(grp), H], U8, name="w1s%d" % g, align_bytes=64) for g, grp in enumerate(W1_PLANES)]
        w1s_of = {e: w1s[g][:, e - grp.start, :] for g, grp in enumerate(W1_PLANES) for e in grp}
        w2w = held.tile([P, E * PASSES, 2 * N], U8, name="w2w", align_bytes=64)
        w2s = held.tile([P, E * PASSES, N], U8, name="w2s", align_bytes=64)
        gate_sb = held.tile([P, SLOTS], F32, name="gate_sb")
        y_sb = held.tile([P, SLOTS], F32, name="y_sb")
        out_sb = held.tile([P, T], F32, name="out_sb")
        ident = held.tile([P, P], F32, name="ident", align_bytes=64)
        zero = held.tile([P, 2], F32, name="zero")

        def load_rows(queue, plane, rows, which):
            for r in which:
                queue.dma_start(out=plane[:].bitcast(I32)[r:P:QUADRANT], in_=rows[r])

        x_rows = x_scales.bitcast(I32)[0].rearrange("(q r) t -> r q t", r=ROWS)
        w2_rows = w2_scales.bitcast(I32).rearrange("e s (q r) n -> r q (e s) n", r=ROWS)
        w1_rows = [
            w1_scales.bitcast(I32)[group.start:group.stop, 0].rearrange("e (q r) i -> r q e i", r=ROWS)
            for group in W1_PLANES
        ]

        def load_w1_words(queue, lo, hi):
            src = w1_words.bitcast(I32)[lo:hi, 0].rearrange("e p b -> p e b")
            queue.dma_start(out=w1w[lo][:].bitcast(I32), in_=src)

        def load_w2_words(queue, lo, hi):
            src = w2_words.bitcast(I32)[lo:hi].rearrange("e s p b -> p (e s) b")
            queue.dma_start(out=w2w[:, lo * PASSES:hi * PASSES, :].bitcast(I32), in_=src)

        def load_gate(queue, lo, hi):
            queue.dma_start(out=gate_sb[:, lo:hi], in_=gate[:, lo:hi])

        nc.vector.memset(tok_scales[:].bitcast(I32), 0)
        nc.vector.memset(zero[:], 0.0)
        nc.vector.memset(w1s[0][:].bitcast(I32), 0)
        nc.vector.memset(w2s[:].bitcast(I32), 0)
        nc.vector.memset(w1s[1][:].bitcast(I32), 0)
        make_identity(nc, ident[:])

        sync.dma_start(offs_sb[:], offs)
        load_gate(sync, 0, WARM_GATES)
        load_w1_words(scalar, 0, 1)
        load_rows(scalar, tok_scales, x_rows, (0, 1,))
        load_rows(sync, tok_scales, x_rows, (2, 3,))
        sync.dma_start(out=tok_words[:], in_=x_words[0].rearrange("p t r -> p (t r)").bitcast(I32))
        load_rows(sync, w1s[0], w1_rows[0], (0, 1,))
        nc.scalar.activation(out=out_sb[:, 0:1536], in_=zero[:, 0:1].to_broadcast([P, 1536]), func=SILU)
        load_rows(scalar, w1s[0], w1_rows[0], (2, 3,))
        load_rows(gpsimd, w2s, w2_rows, (0,))
        load_w1_words(sync, 1, 2)
        load_w1_words(sync, 2, 3)
        load_rows(scalar, w2s, w2_rows, (1,))
        load_rows(sync, w1s[1], w1_rows[1], (0, 1,))
        load_rows(scalar, w1s[1], w1_rows[1], (2, 3,))
        load_rows(scalar, w2s, w2_rows, (2,))
        load_rows(sync, w2s, w2_rows, (3,))
        load_w1_words(sync, 3, 4)
        load_w1_words(sync, 4, 5)
        load_w1_words(sync, 5, 6)
        load_w2_words(sync, 0, 4)
        load_gate(sync, WARM_GATES, 2 * C)
        sync.dma_start(dst_sb[:], dst)
        load_w1_words(sync, 6, 7)
        load_w1_words(sync, 7, 8)
        load_gate(sync, 2 * C, 8 * C)
        load_w2_words(sync, 4, 8)

        slot_words = held.tile([P, SLOTS], U32, name="slot_words", align_bytes=64)
        slot_scales = held.tile([P, SLOTS], U8, name="slot_scales", align_bytes=64)
        arena = ctx.enter_context(tc.tile_pool(name="arena", bufs=1))
        h = {}
        grouped = [held.tile([P, H], BF16, name="grouped%d" % e, align_bytes=64) for e in range(E)]
        scales = [held.tile([P, PASSES * C], U8, name="scales%d" % e, align_bytes=64) for e in range(E)]
        codes = {}
        sums = {}
        turned = {}
        ys = {}
        HELD = {}

        WORDS = ((0, 128, 0), (128, 384, 128), (384, 1024, 384))
        SCALES = ((0, 384, 512), (384, 1024, 0))

        def place(pieces, slot):
            return [at + slot - lo for lo, hi, at in pieces if lo <= slot < hi][0]

        def gather_scales(n):
            lo, hi, at = SCALES[n]
            nc.vector.tensor_copy(slot_scales[:, at:at + hi - lo], tok_scales[:].indirect(offs_sb[:, lo // STRIPE:hi // STRIPE]))

        def gather_words(n):
            lo, hi, at = WORDS[n]
            picks = offs_sb[:, lo // STRIPE:hi // STRIPE]
            nc.vector.tensor_copy(slot_words[:, at:at + hi - lo], tok_words[:].bitcast(U32).indirect(picks))

        def first_matmul(e, s, bank):
            a = psum.tile([P, PASS], F32, name="a%d_%d" % (e, s), offset=bank * BANK)
            nc.tensor.matmul_mx(
                out=a[:],
                lhsT=slot_words[:, place(WORDS, e * C):place(WORDS, e * C) + C].bitcast(FP8X4),
                lhsT_scale=slot_scales[:, place(SCALES, e * C):place(SCALES, e * C) + C],
                rhs=w1w_of[e][:, 2 * s * PASS:2 * (s + 1) * PASS].bitcast(FP4X4),
                rhs_scale=w1s_of[e][:, s * PASS:(s + 1) * PASS],
                start=True,
                stop=True,
            )
            sums[e, s] = a

        def silu(e, s):
            h[e, s] = arena.tile([P, PASS], BF16, name="h%d_%d" % (e, s), align_bytes=64, offset=(e * PASSES + s) * 2 * PASS)
            nc.scalar.activation(
                out=h[e, s][:].rearrange("c (u m d) -> c u m d", u=2, d=2),
                in_=sums[e, s][:].rearrange("c (m u d) -> c u m d", u=2, d=2),
                func=SILU,
            )

        def first(e, s, bank):
            first_matmul(e, s, bank)
            silu(e, s)

        def turn(e, piece, bank):
            tile = psum.tile([P, len(piece), 2, C], F32, name="turned%d_%d" % (e, piece.start), offset=bank * BANK)
            for s in piece:
                pairs = h[e, s][:].bitcast(F32)
                for u in range(2):
                    nc.tensor.transpose(tile[:, s - piece.start, u, :], pairs[:, u * P:(u + 1) * P], ident[:])
            turned[e, piece.start] = tile

        def regroup(engine, e, piece):
            words = grouped[e][:].bitcast(F32)[:, piece.start * 2 * C:piece.stop * 2 * C]
            side_by_side = words.rearrange("p (s c u) -> p s c u", s=len(piece), u=2)
            apart = turned[e, piece.start][:].rearrange("p s u c -> p s c u")
            if engine is nc.scalar:
                nc.scalar.copy(out=side_by_side, in_=apart)
            else:
                nc.vector.tensor_copy(out=side_by_side, in_=apart)

        def quantise(e, piece):
            if e not in codes:
                if e in HELD:
                    codes[e] = arena.tile([P, PASSES * C], U32, name="codes%d" % e, align_bytes=64, offset=HELD[e] * 2 * PASS)
                else:
                    codes[e] = held.tile([P, PASSES * C], U32, name="codes%d" % e, align_bytes=64)
            lo, hi = piece.start * C, piece.stop * C
            nc.vector.quantize_mx(
                out=codes[e][:, lo:hi].bitcast(FP8X4), scales=scales[e][:, lo:hi], in_=grouped[e][:, 4 * lo:4 * hi]
            )

        def second_layer(experts, bank):
            y = psum.tile([P, len(experts) * C], F32, name="y%d" % experts.start, offset=bank * BANK)
            for e in experts:
                place = (e - experts.start) * C
                for s in range(PASSES):
                    nc.tensor.matmul_mx(
                        out=y[:, place:place + C],
                        lhsT=w2w[:, e * PASSES + s, :].bitcast(FP4X4),
                        lhsT_scale=w2s[:, e * PASSES + s, :],
                        rhs=codes[e][:, s * C:(s + 1) * C].bitcast(FP8X4),
                        rhs_scale=scales[e][:, s * C:(s + 1) * C],
                        start=(s == 0),
                        stop=(s == PASSES - 1),
                    )
            ys[experts.start] = y

        def take_y(experts, with_gate=True):
            cols = slice(experts.start * C, experts.stop * C)
            if with_gate:
                nc.vector.tensor_tensor(y_sb[:, cols], ys[experts.start][:], gate_sb[:, cols], MULT)
            else:
                nc.scalar.copy(out=y_sb[:, cols], in_=ys[experts.start][:])

        def scatter(how, lo, hi):
            places = out_sb[:].indirect(dst_sb[:, lo // STRIPE:hi // STRIPE])
            if how == "scalar":
                nc.scalar.activation(places, y_sb[:, lo:hi], COPY)
            elif how == "copy":
                nc.vector.tensor_copy(places, y_sb[:, lo:hi])
            else:
                nc.vector.tensor_tensor(places, y_sb[:, lo:hi], gate_sb[:, lo:hi], MULT)

        both, one, two = range(0, 2), range(0, 1), range(1, 2)
        V, S = nc.vector, nc.scalar
        gather_scales(0)
        gather_words(0)
        gather_words(1)
        gather_words(2)
        first(0, 0, 0)
        first(0, 1, 1)
        first(1, 0, 2)
        first(1, 1, 0)
        turn(0, both, 3)
        regroup(S, 0, both)
        gather_scales(1)
        first(2, 0, 1)
        first(2, 1, 2)
        turn(1, both, 4)
        regroup(V, 1, both)
        quantise(0, both)
        first(3, 0, 0)
        first(3, 1, 1)
        turn(2, both, 5)
        regroup(V, 2, both)
        quantise(1, both)
        first(4, 0, 2)
        first(4, 1, 0)
        turn(3, both, 3)
        regroup(V, 3, both)
        quantise(2, both)
        second_layer(range(0, 2), 6)
        take_y(range(0, 2))
        first(5, 0, 1)
        first(5, 1, 2)
        turn(4, both, 4)
        regroup(S, 4, both)
        quantise(3, both)
        scatter("copy", 0, 256)
        first(6, 0, 0)
        first(6, 1, 1)
        turn(5, both, 5)
        regroup(V, 5, both)
        quantise(4, both)
        second_layer(range(2, 4), 7)
        take_y(range(2, 4))
        first(7, 0, 2)
        first(7, 1, 0)
        turn(6, both, 3)
        regroup(S, 6, both)
        quantise(5, both)
        scatter("copy", 256, 512)
        second_layer(range(4, 5), 1)
        take_y(range(4, 5))
        turn(7, one, 4)
        regroup(S, 7, one)
        turn(7, two, 5)
        regroup(S, 7, two)
        second_layer(range(5, 6), 2)
        take_y(range(5, 6))
        scatter("scalar", 512, 768)
        quantise(6, both)
        quantise(7, one)
        quantise(7, two)
        second_layer(range(6, 7), 6)
        take_y(range(6, 7))
        second_layer(range(7, 8), 7)
        take_y(range(7, 8))
        scatter("scalar", 768, 1024)

        sync.dma_start(out=out, in_=out_sb[:])
